import numpy as np
import ml_dtypes


def mxq(x, axis, fmt="e4m3"):
    dtype, down = {"e4m3": (ml_dtypes.float8_e4m3fn, 7), "e5m2": (ml_dtypes.float8_e5m2, 14)}[fmt]
    v = np.moveaxis(np.asarray(x, np.float32).astype(ml_dtypes.bfloat16).astype(np.float64), axis, -1)
    blocks = v.reshape(v.shape[:-1] + (-1, 32))
    amax = np.abs(blocks).max(-1, keepdims=True)
    byte = np.maximum(np.where(amax > 0, np.frexp(amax)[1] - 1 + 127, 0) - down, 1)
    scale = np.exp2(byte - 127.0)
    codes = (blocks / scale).astype(np.float32).astype(dtype).astype(np.float64)
    return np.moveaxis((codes * scale).reshape(v.shape), -1, axis)


WIDE = False


def mx_kscale(k):
    if not WIDE:
        return np.ones(k)
    levels = np.array([10, -10, 5, -5, 0])
    if k % 512:
        return np.exp2(np.random.permutation(np.resize(levels, k // 32))).repeat(32)
    a = np.empty((k // 512, 16))
    for p in range(k // 512):
        a[p, :8] = np.random.permutation(np.resize(levels, 8))
        for g in range(8):
            far = levels[np.abs(levels - a[p, g]) >= 10]
            a[p, g + 8] = far[np.random.randint(len(far))]
    return np.exp2(a.ravel()).repeat(32)


def f64(x):
    return np.asarray(x).astype(np.float64)


def striped(idx):
    return np.tile(idx.reshape(-1, 16).T, (8, 1)).astype(np.uint16)


def unstriped(offs):
    return offs[:16].T.reshape(-1).astype(np.int64)


E2M1 = np.array([0.0, 0.5, 1.0, 1.5, 2.0, 3.0, 4.0, 6.0, -0.0, -0.5, -1.0, -1.5, -2.0, -3.0, -4.0, -6.0])


def pack_weight(w, fmt):
    k, n = w.shape
    w = f64(np.asarray(w, np.float32).astype(ml_dtypes.bfloat16)).reshape(k // 32, 32, n)
    amax = np.abs(w).max(1)
    if fmt == "e4m3":
        byte = np.frexp(amax)[1] - 1 + 127 - 7
    else:
        mant, ex = np.frexp(amax / 6.0)
        byte = np.where(mant > 0.5, ex, ex - 1) + 127
    byte = np.clip(np.where(amax > 0, byte, 1), 1, 254)
    scaled = (w * np.exp2(127.0 - byte)[:, None, :]).reshape(k, n).astype(np.float32)
    by_word = np.ascontiguousarray(scaled.reshape(k // 512, 128, 4, n).transpose(0, 1, 3, 2))
    if fmt == "e4m3":
        words = by_word.astype(ml_dtypes.float8_e4m3fn).view(np.uint8)
    else:
        c = by_word.astype(ml_dtypes.float4_e2m1fn).view(np.uint8) & 0xF
        words = (c[..., 0::2] | (c[..., 1::2] << 4)).reshape(k // 512, 128, 2 * n)
    return np.ascontiguousarray(words), np.ascontiguousarray(byte.astype(np.uint8).reshape(k // 512, 16, n))


def unpack_weight(words, scales, fmt):
    g, _, n = scales.shape
    words = np.ascontiguousarray(words).reshape(g, 128, n, -1)
    if fmt == "e4m3":
        vals = words.view(ml_dtypes.float8_e4m3fn).astype(np.float64)
    else:
        nib = np.empty((g, 128, n, 4), np.uint8)
        nib[..., 0::2] = words & 0xF
        nib[..., 1::2] = words >> 4
        vals = E2M1[nib]
    vals = vals * np.repeat(np.exp2(scales.astype(np.float64) - 127.0), 8, axis=1)[..., None]
    return vals.transpose(0, 1, 3, 2).reshape(g * 512, n)


def gelu(v):
    return 0.5 * v * (1.0 + np.tanh(np.sqrt(2.0 / np.pi) * (v + 0.044715 * v**3)))


K, H, T, S, T2, S2 = 1024, 1024, 4096, 1024, 1024, 512

def setup_inputs():
    n = np.random.standard_normal
    s = mx_kscale(K)[:, None]
    u = mx_kscale(H)[:, None]
    tab_words, tab_scales = pack_weight(n((K, T)) * s, "e4m3")
    tab2_words, tab2_scales = pack_weight(0.5 * n((H, T2)) / np.sqrt(H) / u, "e4m3")
    w4_words, w4_scales = pack_weight(n((K, H)) / np.sqrt(K) / s * u.T, "e2m1")
    return {
        "tab_words": tab_words, "tab_scales": tab_scales,
        "offs": striped(np.random.permutation(T)[:S]),
        "tab2_words": tab2_words, "tab2_scales": tab2_scales,
        "offs2": striped(np.random.permutation(T2)[:S2]),
        "w1": (n((K, H)) / np.sqrt(K) / s).astype(np.float32),
        "w4_words": w4_words, "w4_scales": w4_scales,
        "pb": (0.4 * n(S2) - 0.5).astype(np.float32),
        "ex": np.exp(0.3 * n(S)).astype(np.float32),
    }

def reference(tab_words, tab_scales, offs, tab2_words, tab2_scales, offs2, w1, w4_words, w4_scales, pb, ex):
    v = unpack_weight(tab_words, tab_scales, "e4m3")[:, unstriped(offs)]
    v2 = unpack_weight(tab2_words, tab2_scales, "e4m3")[:, unstriped(offs2)]
    w4 = unpack_weight(w4_words, w4_scales, "e2m1")
    z = mxq(f64(w1), 0, "e4m3").T @ v
    a = w4.T @ v
    h = a * np.log(1.0 + np.exp(z))
    y = v2.T @ mxq(h, 0, "e4m3")
    return np.exp(y + f64(pb)[:, None]) * f64(ex)[None, :]

@@ -1,0 +1,289 @@
+from contextlib import ExitStack
+
+import concourse.mybir as mybir
+
+F32 = mybir.dt.float32
+BF16 = mybir.dt.bfloat16
+I32 = mybir.dt.int32
+U32 = mybir.dt.uint32
+U16 = mybir.dt.uint16
+U8 = mybir.dt.uint8
+FP8X4 = mybir.dt.float8_e4m3fn_x4
+FP4X4 = mybir.dt.float4_e2m1fn_x4
+ACT = mybir.ActivationFunctionType
+ALU = mybir.AluOpType
+
+K, H, T, S, T2, S2 = 1024, 1024, 4096, 1024, 1024, 512
+FLOPS = 2 * K * H * S * 2 + 2 * H * S2 * S
+
+P = 128
+PACK = 4
+PASS = P * PACK
+PASSES = 2
+BANKS = 8
+QUARTER = 256
+BLOCK = 128
+HALF = 512
+SLIVER = 64
+MOVED = 112
+TINY = 2.0 ** -60
+
+
+def tile_list_claim_count_rates_kernel(
+    tc, tab_words, tab_scales, offs, tab2_words, tab2_scales, offs2, w1, w4_words, w4_scales, pb, ex, out
+):
+    nc = tc.nc
+    with ExitStack() as ctx:
+        keep = ctx.enter_context(tc.tile_pool(name="keep", bufs=1))
+        stage = ctx.enter_context(tc.tile_pool(name="stage", bufs=2))
+        loads = ctx.enter_context(tc.tile_pool(name="loads", bufs=4))
+        psum = ctx.enter_context(tc.psum_pool(name="psum", bufs=1))
+
+        def held(shape, dtype, name):
+            return keep.tile(shape, dtype, name=name, align_bytes=256)
+
+        def bank(k, shape):
+            return psum.tile(shape, F32, name="bank%d" % k)
+
+        holders = keep.tile([P, S // 16], U16, name="holders")
+        perils = keep.tile([P, S2 // 16], U16, name="perils")
+        nc.sync.dma_start(holders[:], offs)
+
+        warm = held([P, 8], F32, "warm")
+        nc.vector.memset(warm[:, 0:1], 0.0)
+        nc.scalar.activation(warm[:, 4:5], warm[:, 0:1], ACT.Sigmoid)
+
+        tab_rows = held([P, T // 4], I32, "tab_rows")
+        w4_rows = held([P, H // 4], I32, "w4_rows")
+        tab2_rows = held([P, T2 // 4], I32, "tab2_rows")
+        v_scale_up = held([P, S // 4], I32, "v_scale_up")
+        w4_scale_up = held([P, H // 4], I32, "w4_scale_up")
+
+        def load_rows(rows, scales):
+            nc.vector.memset(rows[:], 0)
+            for q in range(4):
+                nc.gpsimd.dma_start(rows[32 * q : 32 * q + 8, :], scales.bitcast(I32)[:, 4 * q : 4 * q + 4, :])
+
+        def move_up(dst, src):
+            nc.vector.memset(dst[:], 0)
+            nc.gpsimd.dma_start(dst[0:MOVED, :], src[4 : 4 + MOVED, :].bitcast(I32))
+
+        load_rows(tab_rows, tab_scales)
+        load_rows(w4_rows, w4_scales)
+
+        tab = [held([P, T], I32, "tab%d" % a) for a in range(PASSES)]
+        v_words = [held([P, S], U32, "v_words%d" % a) for a in range(PASSES)]
+        w1_codes = held([P, PASSES, PASSES, PASS], U32, "w1_codes")
+        w1_scale = held([P, PASSES, PASSES, PASS], U8, "w1_scale")
+
+        def load_w1(a, b):
+            raw = loads.tile([P, PACK, PASS], F32, name="w1_raw")
+            rows = w1[a * PASS : (a + 1) * PASS, b * PASS : (b + 1) * PASS]
+            nc.sync.dma_start(raw[:], rows.rearrange("(p j) c -> p j c", j=PACK))
+            return raw
+
+        def load_tab(a):
+            nc.sync.dma_start(tab[a][:], tab_words[a].rearrange("p t i -> p (t i)").bitcast(I32))
+
+        def round_w1(raw, copy):
+            grouped = stage.tile([P, PACK, P, PACK], BF16, name="w1_bf16", align_bytes=256)
+            copy(grouped[:].rearrange("p t m j -> p m j t"), raw[:].rearrange("p j (m t) -> p m j t", t=PACK))
+            return grouped
+
+        def quantize_w1(grouped, a, b):
+            nc.vector.quantize_mx(
+                out=w1_codes[:, b, a, :].bitcast(FP8X4),
+                scales=w1_scale[:, b, a, :],
+                in_=grouped[:].rearrange("p t m j -> p (t m j)"),
+            )
+
+        def gather_v(a, half):
+            nc.vector.tensor_copy(
+                v_words[a][:, half * HALF : (half + 1) * HALF],
+                tab[a][:].bitcast(U32).indirect(holders[:, half * HALF // 16 : (half + 1) * HALF // 16]),
+            )
+
+        raw00 = load_w1(0, 0)
+        load_tab(0)
+        raw10 = load_w1(1, 0)
+        load_tab(1)
+
+        w4_raw = held([P, PASSES, H // 2], I32, "w4_raw")
+        nc.sync.dma_start(w4_raw[:], w4_words.bitcast(I32).rearrange("a p c -> p a c"))
+        raw01 = load_w1(0, 1)
+        raw11 = load_w1(1, 1)
+
+        v_scale = held([P, S], U8, "v_scale")
+        nc.vector.tensor_copy(v_scale[:], tab_rows[:].bitcast(U8).indirect(holders[:]))
+        move_up(v_scale_up, v_scale)
+        w4_scale = held([P, PASSES, PACK, P], U8, "w4_scale")
+        nc.vector.tensor_copy(
+            w4_scale[:].rearrange("p b t m -> p b m t"),
+            w4_rows[:].bitcast(U8).rearrange("p (b m t) -> p b m t", t=PACK, m=P),
+        )
+        move_up(w4_scale_up, w4_scale[:].rearrange("p b t m -> p (b t m)"))
+        load_rows(tab2_rows, tab2_scales)
+
+        quantize_w1(round_w1(raw00, nc.scalar.copy), 0, 0)
+        gather_v(0, 0)
+        gather_v(0, 1)
+        quantize_w1(round_w1(raw10, nc.scalar.copy), 1, 0)
+        gather_v(1, 0)
+        gather_v(1, 1)
+
+        nc.sync.dma_start(perils[:], offs2)
+        tab2 = held([P, PASSES, T2], I32, "tab2")
+        nc.sync.dma_start(tab2[:], tab2_words.rearrange("a p t i -> p a (t i)").bitcast(I32))
+        bias = held([P, S2 // P], F32, "bias")
+        with nc.allow_non_contiguous_dma(reason="one bias value for each partition"):
+            nc.sync.dma_start(bias[:], pb.rearrange("(i p) -> p i", p=P))
+        exposure = held([P, S], F32, "exposure")
+        nc.sync.dma_start(exposure[:], ex.partition_broadcast(P))
+
+        w4_codes = held([P, PASSES, PASSES, PACK, 2 * P], U8, "w4_codes")
+        nc.vector.tensor_copy(
+            w4_codes[:].rearrange("p a b t c -> p (a b t c)").bitcast(U16).rearrange("p (g t m) -> p g m t", t=PACK, m=P),
+            w4_raw[:].rearrange("p a c -> p (a c)").bitcast(U16).rearrange("p (g m t) -> p g m t", t=PACK, m=P),
+        )
+
+        w4_planes = [w4_scale[:].rearrange("p b t m -> p (b t m)"), w4_scale_up[:].bitcast(U8)]
+        v_planes_fp8 = [v_scale[:], v_scale[4:, :]]
+        v_planes_fp4 = [v_scale[:], v_scale_up[:].bitcast(U8)]
+
+        def product(dst, codes, scale, v_planes, first, width):
+            for a in range(PASSES):
+                nc.tensor.matmul_mx(
+                    out=dst,
+                    lhsT=codes(a),
+                    lhsT_scale=scale(a),
+                    rhs=v_words[a][:, first : first + width].bitcast(FP8X4),
+                    rhs_scale=v_planes[a][:, first : first + width],
+                    start=(a == 0),
+                    stop=(a == PASSES - 1),
+                )
+
+        h_codes = held([P, PASSES, S], U32, "h_codes")
+        h_scale = held([P, PASSES, S], U8, "h_scale")
+        v2_words = held([P, PASSES, S2], U32, "v2_words")
+        v2_scale = held([P, S2], U8, "v2_scale")
+        gate = [held([P, BANKS, HALF + SLIVER], F32, "gate%d" % b) for b in range(PASSES)]
+        soft = held([P, BANKS, QUARTER, 2], F32, "soft")
+        h = [held([P, S, PACK], BF16, "h%d" % b) for b in range(PASSES)]
+
+        def gate_of(b, k):
+            if k < BANKS - 1:
+                return gate[b][:, k, 0:HALF].rearrange("p (g n e) -> p g n e", g=BANKS, e=2)
+            return gate[b][:, :, HALF:].rearrange("p g (n e) -> p g n e", e=2)
+
+        def logits(b, k):
+            jq, u = divmod(k, 2)
+            z = bank(k, [P, 2, QUARTER])
+            for e in range(2):
+                t = 2 * u + e
+                cols = slice(t * P, (t + 1) * P)
+                product(
+                    z[:, e, :],
+                    lambda a: w1_codes[:, b, a, cols].bitcast(FP8X4),
+                    lambda a: w1_scale[:, b, a, cols],
+                    v_planes_fp8,
+                    jq * QUARTER,
+                    QUARTER,
+                )
+            z_view = z[:].rearrange("p e (g n) -> p g n e", g=BANKS)
+            nc.scalar.activation(gate_of(b, k), z_view, ACT.Sigmoid, scale=-1.0)
+            return z_view
+
+        def logs(b):
+            for k in range(BANKS):
+                part = gate[b][:, k, :] if k < BANKS - 1 else gate[b][:, k, HALF:]
+                nc.scalar.activation(part, part, ACT.Ln, bias=TINY)
+
+        def softplus(b, k, z_view):
+            nc.vector.scalar_tensor_tensor(
+                soft[:, k].rearrange("p (g n) e -> p g n e", g=BANKS), gate_of(b, k), -1.0, z_view, ALU.mult, ALU.max
+            )
+
+        def linear(b, j):
+            lin = bank(j, [P, PACK, BLOCK])
+            for t in range(PACK):
+                product(
+                    lin[:, t, :],
+                    lambda a: w4_codes[:, a, b, t, :].bitcast(FP4X4),
+                    lambda a: w4_planes[a][:, b * PASS + t * P : b * PASS + (t + 1) * P],
+                    v_planes_fp4,
+                    j * BLOCK,
+                    BLOCK,
+                )
+            return lin
+
+        def gated(b, j, lin):
+            jq, half = divmod(j, 2)
+            nc.vector.tensor_tensor(
+                h[b][:, j * BLOCK : (j + 1) * BLOCK, :].rearrange("p n (u e) -> p n u e", e=2),
+                lin[:].rearrange("p (u e) n -> p n u e", e=2),
+                soft[:, 2 * jq : 2 * jq + 2, half * BLOCK : (half + 1) * BLOCK, :].rearrange("p u n e -> p n u e"),
+                ALU.mult,
+            )
+
+        def quantize_h(b, first, width):
+            nc.vector.quantize_mx(
+                out=h_codes[:, b, first : first + width].bitcast(FP8X4),
+                scales=h_scale[:, b, first : first + width],
+                in_=h[b][:, first : first + width, :].rearrange("p n t -> p (n t)"),
+            )
+
+        def rates(jq):
+            cols = slice(jq * QUARTER, (jq + 1) * QUARTER)
+            counts = held([P, PACK, QUARTER], F32, "counts%d" % jq)
+            for pair in range(2):
+                y = bank(2 * jq + pair, [P, 2, QUARTER])
+                for e in range(2):
+                    i = 2 * pair + e
+                    for b in range(PASSES):
+                        nc.tensor.matmul_mx(
+                            out=y[:, e, :],
+                            lhsT=v2_words[:, b, i * P : (i + 1) * P].bitcast(FP8X4),
+                            lhsT_scale=v2_scale[4 * b :, i * P : (i + 1) * P],
+                            rhs=h_codes[:, b, cols].bitcast(FP8X4),
+                            rhs_scale=h_scale[:, b, cols],
+                            start=(b == 0),
+                            stop=(b == PASSES - 1),
+                        )
+                for e in range(2):
+                    i = 2 * pair + e
+                    nc.scalar.activation(counts[:, i, :], y[:, e, :], ACT.Exp, bias=bias[:, i : i + 1])
+                part = counts[:, 2 * pair : 2 * pair + 2, :]
+                nc.vector.tensor_tensor(
+                    part, part, exposure[:, cols].unsqueeze(1).to_broadcast([P, 2, QUARTER]), ALU.mult
+                )
+                nc.sync.dma_start(
+                    out[2 * pair * P : (2 * pair + 2) * P, cols].rearrange("(i p) n -> p i n", p=P), part
+                )
+
+        z_views = [logits(0, k) for k in range(BANKS)]
+        quantize_w1(round_w1(raw01, nc.vector.tensor_copy), 0, 1)
+        quantize_w1(round_w1(raw11, nc.vector.tensor_copy), 1, 1)
+
+        for b in range(PASSES):
+            logs(b)
+            lins = {}
+            next_views = []
+            for step in range(BANKS + 2):
+                if step < BANKS:
+                    softplus(b, step, z_views[step])
+                    lins[step] = linear(b, step)
+                j = step - 2
+                if j >= 0:
+                    gated(b, j, lins[j])
+                    if b == 0:
+                        next_views.append(logits(1, j))
+                    elif j % 2 == 1:
+                        quantize_h(b, (j // 2) * QUARTER, QUARTER)
+                        rates(j // 2)
+            if b == 0:
+                for half in range(2):
+                    quantize_h(0, half * HALF, HALF)
+                for c in range(PASSES):
+                    nc.vector.tensor_copy(v2_words[:, c, :], tab2[:, c, :].bitcast(U32).indirect(perils[:]))
+                nc.vector.tensor_copy(v2_scale[:], tab2_rows[:].bitcast(U8).indirect(perils[:]))
+            z_views = next_views

@@ -25,7 +25,6 @@ QUARTER = 256
 BLOCK = 128
 HALF = 512
 SLIVER = 64
-MOVED = 112
 TINY = 2.0 ** -60
 
 
@@ -36,7 +35,6 @@ def tile_list_claim_count_rates_kernel(
     with ExitStack() as ctx:
         keep = ctx.enter_context(tc.tile_pool(name="keep", bufs=1))
         stage = ctx.enter_context(tc.tile_pool(name="stage", bufs=2))
-        loads = ctx.enter_context(tc.tile_pool(name="loads", bufs=4))
         psum = ctx.enter_context(tc.psum_pool(name="psum", bufs=1))
 
         def held(shape, dtype, name):
@@ -49,27 +47,15 @@ def tile_list_claim_count_rates_kernel(
         perils = keep.tile([P, S2 // 16], U16, name="perils")
         nc.sync.dma_start(holders[:], offs)
 
+        tab_rows = held([P, T // 4], I32, "tab_rows")
+        nc.vector.memset(tab_rows[:], 0)
         warm = held([P, 8], F32, "warm")
         nc.vector.memset(warm[:, 0:1], 0.0)
         nc.scalar.activation(warm[:, 4:5], warm[:, 0:1], ACT.Sigmoid)
 
-        tab_rows = held([P, T // 4], I32, "tab_rows")
-        w4_rows = held([P, H // 4], I32, "w4_rows")
+        w4_rows = held([P, PASSES, H // 4], I32, "w4_rows")
         tab2_rows = held([P, T2 // 4], I32, "tab2_rows")
-        v_scale_up = held([P, S // 4], I32, "v_scale_up")
-        w4_scale_up = held([P, H // 4], I32, "w4_scale_up")
-
-        def load_rows(rows, scales):
-            nc.vector.memset(rows[:], 0)
-            for q in range(4):
-                nc.gpsimd.dma_start(rows[32 * q : 32 * q + 8, :], scales.bitcast(I32)[:, 4 * q : 4 * q + 4, :])
-
-        def move_up(dst, src):
-            nc.vector.memset(dst[:], 0)
-            nc.gpsimd.dma_start(dst[0:MOVED, :], src[4 : 4 + MOVED, :].bitcast(I32))
-
-        load_rows(tab_rows, tab_scales)
-        load_rows(w4_rows, w4_scales)
+        v_scale = held([P, PASSES, S // 4], I32, "v_scale")
 
         tab = [held([P, T], I32, "tab%d" % a) for a in range(PASSES)]
         v_words = [held([P, S], U32, "v_words%d" % a) for a in range(PASSES)]
@@ -77,7 +63,7 @@ def tile_list_claim_count_rates_kernel(
         w1_scale = held([P, PASSES, PASSES, PASS], U8, "w1_scale")
 
         def load_w1(a, b):
-            raw = loads.tile([P, PACK, PASS], F32, name="w1_raw")
+            raw = stage.tile([P, PACK, PASS], F32, name="w1_raw")
             rows = w1[a * PASS : (a + 1) * PASS, b * PASS : (b + 1) * PASS]
             nc.sync.dma_start(raw[:], rows.rearrange("(p j) c -> p j c", j=PACK))
             return raw
@@ -103,37 +89,48 @@ def tile_list_claim_count_rates_kernel(
                 tab[a][:].bitcast(U32).indirect(holders[:, half * HALF // 16 : (half + 1) * HALF // 16]),
             )
 
+        picked_rows = held([P, S], U8, "picked_rows")
+
+        def move_rows(a):
+            for q in range(4):
+                first = 64 * a + 16 * q
+                nc.sync.dma_start(
+                    v_scale[32 * q : 32 * q + 4, a, :], picked_rows[first : first + 16 : 4, :].bitcast(I32)
+                )
+
         raw00 = load_w1(0, 0)
+        nc.sync.dma_start(tab_rows[0:P:4, :], tab_scales.rearrange("a q t -> (a q) t").bitcast(I32))
         load_tab(0)
         raw10 = load_w1(1, 0)
+        nc.vector.memset(v_scale[:], 0)
+        nc.vector.tensor_copy(picked_rows[:], tab_rows[:].bitcast(U8).indirect(holders[:]))
+        move_rows(0)
         load_tab(1)
-
-        w4_raw = held([P, PASSES, H // 2], I32, "w4_raw")
-        nc.sync.dma_start(w4_raw[:], w4_words.bitcast(I32).rearrange("a p c -> p a c"))
-        raw01 = load_w1(0, 1)
-        raw11 = load_w1(1, 1)
-
-        v_scale = held([P, S], U8, "v_scale")
-        nc.vector.tensor_copy(v_scale[:], tab_rows[:].bitcast(U8).indirect(holders[:]))
-        move_up(v_scale_up, v_scale)
-        w4_scale = held([P, PASSES, PACK, P], U8, "w4_scale")
-        nc.vector.tensor_copy(
-            w4_scale[:].rearrange("p b t m -> p b m t"),
-            w4_rows[:].bitcast(U8).rearrange("p (b m t) -> p b m t", t=PACK, m=P),
-        )
-        move_up(w4_scale_up, w4_scale[:].rearrange("p b t m -> p (b t m)"))
-        load_rows(tab2_rows, tab2_scales)
+        move_rows(1)
 
         quantize_w1(round_w1(raw00, nc.scalar.copy), 0, 0)
+        raw01 = load_w1(0, 1)
         gather_v(0, 0)
         gather_v(0, 1)
         quantize_w1(round_w1(raw10, nc.scalar.copy), 1, 0)
+        raw11 = load_w1(1, 1)
         gather_v(1, 0)
         gather_v(1, 1)
 
+        w4_raw = held([P, PASSES, H // 2], I32, "w4_raw")
+        nc.sync.dma_start(w4_raw[:], w4_words.bitcast(I32).rearrange("a p c -> p a c"))
+        nc.vector.memset(w4_rows[:], 0)
+        for q in range(4):
+            nc.sync.dma_start(
+                w4_rows[32 * q : 32 * q + 4, :, :],
+                w4_scales.bitcast(I32)[:, 4 * q : 4 * q + 4, :].rearrange("a r c -> r a c"),
+            )
         nc.sync.dma_start(perils[:], offs2)
         tab2 = held([P, PASSES, T2], I32, "tab2")
         nc.sync.dma_start(tab2[:], tab2_words.rearrange("a p t i -> p a (t i)").bitcast(I32))
+        nc.vector.memset(tab2_rows[:], 0)
+        for q in range(4):
+            nc.sync.dma_start(tab2_rows[32 * q : 32 * q + 8, :], tab2_scales.bitcast(I32)[:, 4 * q : 4 * q + 4, :])
         bias = held([P, S2 // P], F32, "bias")
         with nc.allow_non_contiguous_dma(reason="one bias value for each partition"):
             nc.sync.dma_start(bias[:], pb.rearrange("(i p) -> p i", p=P))
@@ -141,16 +138,21 @@ def tile_list_claim_count_rates_kernel(
         nc.sync.dma_start(exposure[:], ex.partition_broadcast(P))
 
         w4_codes = held([P, PASSES, PASSES, PACK, 2 * P], U8, "w4_codes")
-        nc.vector.tensor_copy(
-            w4_codes[:].rearrange("p a b t c -> p (a b t c)").bitcast(U16).rearrange("p (g t m) -> p g m t", t=PACK, m=P),
-            w4_raw[:].rearrange("p a c -> p (a c)").bitcast(U16).rearrange("p (g m t) -> p g m t", t=PACK, m=P),
-        )
+        w4_scale = held([P, PASSES, PASSES, PACK, P], U8, "w4_scale")
 
-        w4_planes = [w4_scale[:].rearrange("p b t m -> p (b t m)"), w4_scale_up[:].bitcast(U8)]
-        v_planes_fp8 = [v_scale[:], v_scale[4:, :]]
-        v_planes_fp4 = [v_scale[:], v_scale_up[:].bitcast(U8)]
+        def permute_w4():
+            nc.vector.tensor_copy(
+                w4_codes[:].rearrange("p a b t c -> p (a b t c)").bitcast(U16).rearrange("p (g t m) -> p g m t", t=PACK, m=P),
+                w4_raw[:].rearrange("p a c -> p (a c)").bitcast(U16).rearrange("p (g m t) -> p g m t", t=PACK, m=P),
+            )
+            nc.vector.tensor_copy(
+                w4_scale[:].rearrange("p a b t m -> p (a b) m t"),
+                w4_rows[:].rearrange("p a c -> p (a c)").bitcast(U8).rearrange("p (g m t) -> p g m t", t=PACK, m=P),
+            )
 
-        def product(dst, codes, scale, v_planes, first, width):
+        v_planes = [v_scale[:, a, :].bitcast(U8) for a in range(PASSES)]
+
+        def product(dst, codes, scale, first, width):
             for a in range(PASSES):
                 nc.tensor.matmul_mx(
                     out=dst,
@@ -185,7 +187,6 @@ def tile_list_claim_count_rates_kernel(
                     z[:, e, :],
                     lambda a: w1_codes[:, b, a, cols].bitcast(FP8X4),
                     lambda a: w1_scale[:, b, a, cols],
-                    v_planes_fp8,
                     jq * QUARTER,
                     QUARTER,
                 )
@@ -209,8 +210,7 @@ def tile_list_claim_count_rates_kernel(
                 product(
                     lin[:, t, :],
                     lambda a: w4_codes[:, a, b, t, :].bitcast(FP4X4),
-                    lambda a: w4_planes[a][:, b * PASS + t * P : b * PASS + (t + 1) * P],
-                    v_planes_fp4,
+                    lambda a: w4_scale[:, a, b, t, :],
                     j * BLOCK,
                     BLOCK,
                 )
@@ -252,8 +252,13 @@ def tile_list_claim_count_rates_kernel(
                 for e in range(2):
                     i = 2 * pair + e
                     nc.scalar.activation(counts[:, i, :], y[:, e, :], ACT.Exp, bias=bias[:, i : i + 1])
+            return counts
+
+        def expose(jq, counts, engine):
+            cols = slice(jq * QUARTER, (jq + 1) * QUARTER)
+            for pair in range(2):
                 part = counts[:, 2 * pair : 2 * pair + 2, :]
-                nc.vector.tensor_tensor(
+                engine.tensor_tensor(
                     part, part, exposure[:, cols].unsqueeze(1).to_broadcast([P, 2, QUARTER]), ALU.mult
                 )
                 nc.sync.dma_start(
@@ -263,27 +268,35 @@ def tile_list_claim_count_rates_kernel(
         z_views = [logits(0, k) for k in range(BANKS)]
         quantize_w1(round_w1(raw01, nc.vector.tensor_copy), 0, 1)
         quantize_w1(round_w1(raw11, nc.vector.tensor_copy), 1, 1)
+        permute_w4()
 
-        for b in range(PASSES):
-            logs(b)
-            lins = {}
-            next_views = []
-            for step in range(BANKS + 2):
-                if step < BANKS:
-                    softplus(b, step, z_views[step])
-                    lins[step] = linear(b, step)
-                j = step - 2
-                if j >= 0:
-                    gated(b, j, lins[j])
-                    if b == 0:
-                        next_views.append(logits(1, j))
-                    elif j % 2 == 1:
-                        quantize_h(b, (j // 2) * QUARTER, QUARTER)
-                        rates(j // 2)
-            if b == 0:
-                for half in range(2):
-                    quantize_h(0, half * HALF, HALF)
-                for c in range(PASSES):
-                    nc.vector.tensor_copy(v2_words[:, c, :], tab2[:, c, :].bitcast(U32).indirect(perils[:]))
-                nc.vector.tensor_copy(v2_scale[:], tab2_rows[:].bitcast(U8).indirect(perils[:]))
-            z_views = next_views
+        logs(0)
+        lins = []
+        for k in range(BANKS):
+            softplus(0, k, z_views[k])
+            lins.append(linear(0, k))
+        z_views = []
+        for j in range(BANKS):
+            gated(0, j, lins[j])
+            z_views.append(logits(1, j))
+        for half in range(2):
+            quantize_h(0, half * HALF, HALF)
+        for c in range(PASSES):
+            nc.vector.tensor_copy(v2_words[:, c, :], tab2[:, c, :].bitcast(U32).indirect(perils[:]))
+        nc.vector.tensor_copy(v2_scale[:], tab2_rows[:].bitcast(U8).indirect(perils[:]))
+
+        logs(1)
+        lins = []
+        done = []
+        for step in range(BANKS + 2):
+            if step < BANKS:
+                softplus(1, step, z_views[step])
+                lins.append(linear(1, step))
+            j = step - 2
+            if j >= 0:
+                gated(1, j, lins[j])
+                if j % 2 == 1:
+                    quantize_h(1, (j // 2) * QUARTER, QUARTER)
+                    done.append(rates(j // 2))
+        for jq, counts in enumerate(done):
+            expose(jq, counts, nc.gpsimd if jq < 2 else nc.vector)

@@ -34,7 +34,6 @@ def tile_list_claim_count_rates_kernel(
     nc = tc.nc
     with ExitStack() as ctx:
         keep = ctx.enter_context(tc.tile_pool(name="keep", bufs=1))
-        stage = ctx.enter_context(tc.tile_pool(name="stage", bufs=2))
         psum = ctx.enter_context(tc.psum_pool(name="psum", bufs=1))
 
         def held(shape, dtype, name):
@@ -63,7 +62,7 @@ def tile_list_claim_count_rates_kernel(
         w1_scale = held([P, PASSES, PASSES, PASS], U8, "w1_scale")
 
         def load_w1(a, b):
-            raw = stage.tile([P, PACK, PASS], F32, name="w1_raw")
+            raw = keep.tile([P, PACK, PASS], F32, name="w1_raw", tag="shared%d" % a)
             rows = w1[a * PASS : (a + 1) * PASS, b * PASS : (b + 1) * PASS]
             nc.sync.dma_start(raw[:], rows.rearrange("(p j) c -> p j c", j=PACK))
             return raw
@@ -71,17 +70,17 @@ def tile_list_claim_count_rates_kernel(
         def load_tab(a):
             nc.sync.dma_start(tab[a][:], tab_words[a].rearrange("p t i -> p (t i)").bitcast(I32))
 
-        def round_w1(raw, copy):
-            grouped = stage.tile([P, PACK, P, PACK], BF16, name="w1_bf16", align_bytes=256)
-            copy(grouped[:].rearrange("p t m j -> p m j t"), raw[:].rearrange("p j (m t) -> p m j t", t=PACK))
-            return grouped
+        def round_w1(raw, grouped, copy):
+            copy(grouped.rearrange("p t m j -> p m j t"), raw[:].rearrange("p j (m t) -> p m j t", t=PACK))
 
-        def quantize_w1(grouped, a, b):
+        def quantize_w1(grouped, b):
             nc.vector.quantize_mx(
-                out=w1_codes[:, b, a, :].bitcast(FP8X4),
-                scales=w1_scale[:, b, a, :],
-                in_=grouped[:].rearrange("p t m j -> p (t m j)"),
+                out=w1_codes[:, b].rearrange("p a c -> p (a c)").bitcast(FP8X4),
+                scales=w1_scale[:, b].rearrange("p a c -> p (a c)"),
+                in_=grouped[:].rearrange("p a t m j -> p (a t m j)"),
             )
+
+        w1_bf16 = [held([P, PASSES, PACK, P, PACK], BF16, "w1_bf16_%d" % b) for b in range(PASSES)]
 
         def gather_v(a, half):
             nc.vector.tensor_copy(
@@ -108,23 +107,24 @@ def tile_list_claim_count_rates_kernel(
         load_tab(1)
         move_rows(1)
 
-        quantize_w1(round_w1(raw00, nc.scalar.copy), 0, 0)
-        raw01 = load_w1(0, 1)
-        gather_v(0, 0)
-        gather_v(0, 1)
-        quantize_w1(round_w1(raw10, nc.scalar.copy), 1, 0)
-        raw11 = load_w1(1, 1)
-        gather_v(1, 0)
-        gather_v(1, 1)
-
         w4_raw = held([P, PASSES, H // 2], I32, "w4_raw")
         nc.sync.dma_start(w4_raw[:], w4_words.bitcast(I32).rearrange("a p c -> p a c"))
+        round_w1(raw00, w1_bf16[0][:, 0], nc.scalar.copy)
+        raw01 = load_w1(0, 1)
         nc.vector.memset(w4_rows[:], 0)
         for q in range(4):
             nc.sync.dma_start(
                 w4_rows[32 * q : 32 * q + 4, :, :],
                 w4_scales.bitcast(I32)[:, 4 * q : 4 * q + 4, :].rearrange("a r c -> r a c"),
             )
+        gather_v(0, 0)
+        gather_v(0, 1)
+        round_w1(raw10, w1_bf16[0][:, 1], nc.scalar.copy)
+        quantize_w1(w1_bf16[0], 0)
+        raw11 = load_w1(1, 1)
+        gather_v(1, 0)
+        gather_v(1, 1)
+
         nc.sync.dma_start(perils[:], offs2)
         tab2 = held([P, PASSES, T2], I32, "tab2")
         nc.sync.dma_start(tab2[:], tab2_words.rearrange("a p t i -> p a (t i)").bitcast(I32))
@@ -140,11 +140,13 @@ def tile_list_claim_count_rates_kernel(
         w4_codes = held([P, PASSES, PASSES, PACK, 2 * P], U8, "w4_codes")
         w4_scale = held([P, PASSES, PASSES, PACK, P], U8, "w4_scale")
 
-        def permute_w4():
+        def permute_w4_codes():
             nc.vector.tensor_copy(
                 w4_codes[:].rearrange("p a b t c -> p (a b t c)").bitcast(U16).rearrange("p (g t m) -> p g m t", t=PACK, m=P),
                 w4_raw[:].rearrange("p a c -> p (a c)").bitcast(U16).rearrange("p (g m t) -> p g m t", t=PACK, m=P),
             )
+
+        def permute_w4_scales():
             nc.vector.tensor_copy(
                 w4_scale[:].rearrange("p a b t m -> p (a b) m t"),
                 w4_rows[:].rearrange("p a c -> p (a c)").bitcast(U8).rearrange("p (g m t) -> p g m t", t=PACK, m=P),
@@ -169,7 +171,6 @@ def tile_list_claim_count_rates_kernel(
         v2_words = held([P, PASSES, S2], U32, "v2_words")
         v2_scale = held([P, S2], U8, "v2_scale")
         gate = [held([P, BANKS, HALF + SLIVER], F32, "gate%d" % b) for b in range(PASSES)]
-        soft = held([P, BANKS, QUARTER, 2], F32, "soft")
         h = [held([P, S, PACK], BF16, "h%d" % b) for b in range(PASSES)]
 
         def gate_of(b, k):
@@ -232,13 +233,14 @@ def tile_list_claim_count_rates_kernel(
                 in_=h[b][:, first : first + width, :].rearrange("p n t -> p (n t)"),
             )
 
-        def rates(jq):
-            cols = slice(jq * QUARTER, (jq + 1) * QUARTER)
-            counts = held([P, PACK, QUARTER], F32, "counts%d" % jq)
-            for pair in range(2):
-                y = bank(2 * jq + pair, [P, 2, QUARTER])
-                for e in range(2):
-                    i = 2 * pair + e
+        def rates(first, width):
+            cols = slice(first, first + width)
+            tiles_in_bank = HALF // width
+            counts = held([P, PACK, width], F32, "counts%d" % first)
+            for group in range(PACK // tiles_in_bank):
+                y = bank(first // BLOCK + group, [P, tiles_in_bank, width])
+                for e in range(tiles_in_bank):
+                    i = tiles_in_bank * group + e
                     for b in range(PASSES):
                         nc.tensor.matmul_mx(
                             out=y[:, e, :],
@@ -249,26 +251,30 @@ def tile_list_claim_count_rates_kernel(
                             start=(b == 0),
                             stop=(b == PASSES - 1),
                         )
-                for e in range(2):
-                    i = 2 * pair + e
+                for e in range(tiles_in_bank):
+                    i = tiles_in_bank * group + e
                     nc.scalar.activation(counts[:, i, :], y[:, e, :], ACT.Exp, bias=bias[:, i : i + 1])
             return counts
 
-        def expose(jq, counts, engine):
-            cols = slice(jq * QUARTER, (jq + 1) * QUARTER)
-            for pair in range(2):
-                part = counts[:, 2 * pair : 2 * pair + 2, :]
-                engine.tensor_tensor(
-                    part, part, exposure[:, cols].unsqueeze(1).to_broadcast([P, 2, QUARTER]), ALU.mult
-                )
-                nc.sync.dma_start(
-                    out[2 * pair * P : (2 * pair + 2) * P, cols].rearrange("(i p) n -> p i n", p=P), part
-                )
+        def expose(first, width, counts, engine, tiles, stored, queue):
+            cols = slice(first, first + width)
+            for i in range(0, PACK, tiles):
+                part = counts[:, i : i + tiles, :]
+                engine.tensor_tensor(part, part, exposure[:, cols].unsqueeze(1).to_broadcast([P, tiles, width]), ALU.mult)
+                if (i + tiles) % stored == 0:
+                    low = i + tiles - stored
+                    queue.dma_start(
+                        out[low * P : (low + stored) * P, cols].rearrange("(i p) n -> p i n", p=P),
+                        counts[:, low : low + stored, :],
+                    )
 
         z_views = [logits(0, k) for k in range(BANKS)]
-        quantize_w1(round_w1(raw01, nc.vector.tensor_copy), 0, 1)
-        quantize_w1(round_w1(raw11, nc.vector.tensor_copy), 1, 1)
-        permute_w4()
+        permute_w4_codes()
+        round_w1(raw01, w1_bf16[1][:, 0], nc.vector.tensor_copy)
+        round_w1(raw11, w1_bf16[1][:, 1], nc.vector.tensor_copy)
+        permute_w4_scales()
+        quantize_w1(w1_bf16[1], 1)
+        soft = keep.tile([P, BANKS, QUARTER, 2], F32, name="soft", tag="shared1")
 
         logs(0)
         lins = []
@@ -287,16 +293,27 @@ def tile_list_claim_count_rates_kernel(
 
         logs(1)
         lins = []
+        pieces = [(0, QUARTER), (QUARTER, QUARTER), (2 * QUARTER, QUARTER), (6 * BLOCK, BLOCK), (7 * BLOCK, BLOCK)]
         done = []
-        for step in range(BANKS + 2):
-            if step < BANKS:
-                softplus(1, step, z_views[step])
-                lins.append(linear(1, step))
-            j = step - 2
-            if j >= 0:
-                gated(1, j, lins[j])
-                if j % 2 == 1:
-                    quantize_h(1, (j // 2) * QUARTER, QUARTER)
-                    done.append(rates(j // 2))
-        for jq, counts in enumerate(done):
-            expose(jq, counts, nc.gpsimd if jq < 2 else nc.vector)
+
+        def finish(piece):
+            quantize_h(1, *pieces[piece])
+            done.append(rates(*pieces[piece]))
+
+        for step in range(BANKS):
+            softplus(1, step, z_views[step])
+            lins.append(linear(1, step))
+            if step in (4, 6):
+                finish(step // 2 - 2)
+            if step >= 2:
+                gated(1, step - 2, lins[step - 2])
+        gated(1, 6, lins[6])
+        finish(2)
+        gated(1, 7, lins[7])
+        finish(3)
+        finish(4)
+        for piece in range(2):
+            expose(*pieces[piece], done[piece], nc.gpsimd, 1, 2, nc.sync)
+        expose(*pieces[2], done[2], nc.vector, 2, 2, nc.scalar)
+        expose(*pieces[3], done[3], nc.vector, 4, 4, nc.scalar)
+        expose(*pieces[4], done[4], nc.vector, 2, 2, nc.scalar)

@@ -71,7 +71,7 @@ def tile_list_claim_count_rates_kernel(
             nc.sync.dma_start(tab[a][:], tab_words[a].rearrange("p t i -> p (t i)").bitcast(I32))
 
         def round_w1(raw, grouped, copy):
-            copy(grouped.rearrange("p t m j -> p m j t"), raw[:].rearrange("p j (m t) -> p m j t", t=PACK))
+            copy(grouped.rearrange("p t m j -> p m t j"), raw[:].rearrange("p j (m t) -> p m t j", t=PACK))
 
         def quantize_w1(grouped, b):
             nc.vector.quantize_mx(
@@ -140,16 +140,24 @@ def tile_list_claim_count_rates_kernel(
         w4_codes = held([P, PASSES, PASSES, PACK, 2 * P], U8, "w4_codes")
         w4_scale = held([P, PASSES, PASSES, PACK, P], U8, "w4_scale")
 
-        def permute_w4_codes():
+        def permute(dst, src, run):
             nc.vector.tensor_copy(
-                w4_codes[:].rearrange("p a b t c -> p (a b t c)").bitcast(U16).rearrange("p (g t m) -> p g m t", t=PACK, m=P),
-                w4_raw[:].rearrange("p a c -> p (a c)").bitcast(U16).rearrange("p (g m t) -> p g m t", t=PACK, m=P),
+                dst.rearrange("p (g t m i) -> p g m t i", t=PACK, m=P // run, i=run),
+                src.rearrange("p (g m i t) -> p g m t i", t=PACK, m=P // run, i=run),
+            )
+
+        def permute_w4_codes():
+            permute(
+                w4_codes[:].rearrange("p a b t c -> p (a b t c)").bitcast(U16),
+                w4_raw[:].rearrange("p a c -> p (a c)").bitcast(U16),
+                8,
             )
 
         def permute_w4_scales():
-            nc.vector.tensor_copy(
-                w4_scale[:].rearrange("p a b t m -> p (a b) m t"),
-                w4_rows[:].rearrange("p a c -> p (a c)").bitcast(U8).rearrange("p (g m t) -> p g m t", t=PACK, m=P),
+            permute(
+                w4_scale[:].rearrange("p a b t m -> p (a b t m)"),
+                w4_rows[:].rearrange("p a c -> p (a c)").bitcast(U8),
+                16,
             )
 
         v_planes = [v_scale[:, a, :].bitcast(U8) for a in range(PASSES)]
@@ -256,9 +264,9 @@ def tile_list_claim_count_rates_kernel(
                     nc.scalar.activation(counts[:, i, :], y[:, e, :], ACT.Exp, bias=bias[:, i : i + 1])
             return counts
 
-        def expose(first, width, counts, engine, tiles, stored, queue):
+        def expose(first, width, counts, engine, tiles, stored, queue, low_tile=0, high_tile=PACK):
             cols = slice(first, first + width)
-            for i in range(0, PACK, tiles):
+            for i in range(low_tile, high_tile, tiles):
                 part = counts[:, i : i + tiles, :]
                 engine.tensor_tensor(part, part, exposure[:, cols].unsqueeze(1).to_broadcast([P, tiles, width]), ALU.mult)
                 if (i + tiles) % stored == 0:
@@ -312,8 +320,9 @@ def tile_list_claim_count_rates_kernel(
         gated(1, 7, lins[7])
         finish(3)
         finish(4)
-        for piece in range(2):
-            expose(*pieces[piece], done[piece], nc.gpsimd, 1, 2, nc.sync)
+        expose(*pieces[0], done[0], nc.gpsimd, 1, 2, nc.sync)
+        expose(*pieces[1], done[1], nc.gpsimd, 1, 2, nc.sync, 0, 2)
+        expose(*pieces[1], done[1], nc.vector, 2, 2, nc.sync, 2, 4)
         expose(*pieces[2], done[2], nc.vector, 2, 2, nc.scalar)
         expose(*pieces[3], done[3], nc.vector, 4, 4, nc.scalar)
         expose(*pieces[4], done[4], nc.vector, 2, 2, nc.scalar)

@@ -25,6 +25,7 @@ QUARTER = 256
 BLOCK = 128
 HALF = 512
 SLIVER = 64
+PARKED = 2
 TINY = 2.0 ** -60
 
 
@@ -44,7 +45,6 @@ def tile_list_claim_count_rates_kernel(
 
         holders = keep.tile([P, S // 16], U16, name="holders")
         perils = keep.tile([P, S2 // 16], U16, name="perils")
-        nc.sync.dma_start(holders[:], offs)
 
         tab_rows = held([P, T // 4], I32, "tab_rows")
         nc.vector.memset(tab_rows[:], 0)
@@ -98,6 +98,7 @@ def tile_list_claim_count_rates_kernel(
                 )
 
         raw00 = load_w1(0, 0)
+        nc.sync.dma_start(holders[:], offs)
         nc.sync.dma_start(tab_rows[0:P:4, :], tab_scales.rearrange("a q t -> (a q) t").bitcast(I32))
         load_tab(0)
         raw10 = load_w1(1, 0)
@@ -188,7 +189,7 @@ def tile_list_claim_count_rates_kernel(
 
         def logits(b, k):
             jq, u = divmod(k, 2)
-            z = bank(k, [P, 2, QUARTER])
+            z = bank((k - b * PARKED) % BANKS, [P, 2, QUARTER])
             for e in range(2):
                 t = 2 * u + e
                 cols = slice(t * P, (t + 1) * P)
@@ -214,7 +215,7 @@ def tile_list_claim_count_rates_kernel(
             )
 
         def linear(b, j):
-            lin = bank(j, [P, PACK, BLOCK])
+            lin = bank((j - PARKED) % BANKS, [P, PACK, BLOCK])
             for t in range(PACK):
                 product(
                     lin[:, t, :],
@@ -246,7 +247,7 @@ def tile_list_claim_count_rates_kernel(
             tiles_in_bank = HALF // width
             counts = held([P, PACK, width], F32, "counts%d" % first)
             for group in range(PACK // tiles_in_bank):
-                y = bank(first // BLOCK + group, [P, tiles_in_bank, width])
+                y = bank((first // BLOCK + group - PARKED) % BANKS, [P, tiles_in_bank, width])
                 for e in range(tiles_in_bank):
                     i = tiles_in_bank * group + e
                     for b in range(PASSES):
@@ -276,19 +277,27 @@ def tile_list_claim_count_rates_kernel(
                         counts[:, low : low + stored, :],
                     )
 
-        z_views = [logits(0, k) for k in range(BANKS)]
+        z_views = [logits(0, k) for k in range(BANKS - 1)]
+        parked = held([P, BANKS, SLIVER // 2, 2], F32, "parked")
+        nc.scalar.copy(parked[:], z_views[BANKS - 2])
+        z_views[BANKS - 2] = parked[:]
+        z_views.append(logits(0, BANKS - 1))
         permute_w4_codes()
         round_w1(raw01, w1_bf16[1][:, 0], nc.vector.tensor_copy)
         round_w1(raw11, w1_bf16[1][:, 1], nc.vector.tensor_copy)
         permute_w4_scales()
-        quantize_w1(w1_bf16[1], 1)
         soft = keep.tile([P, BANKS, QUARTER, 2], F32, name="soft", tag="shared1")
+        last = soft[:, BANKS - 1].rearrange("p (g n) e -> p g n e", g=BANKS)
+        nc.vector.tensor_copy(last, z_views[BANKS - 1])
+        z_views[BANKS - 1] = last
+        quantize_w1(w1_bf16[1], 1)
 
         logs(0)
-        lins = []
+        lins = [linear(0, j) for j in range(PARKED)]
         for k in range(BANKS):
             softplus(0, k, z_views[k])
-            lins.append(linear(0, k))
+            if k + PARKED < BANKS:
+                lins.append(linear(0, k + PARKED))
         z_views = []
         for j in range(BANKS):
             gated(0, j, lins[j])

@@ -25,8 +25,12 @@ QUARTER = 256
 BLOCK = 128
 HALF = 512
 SLIVER = 64
-PARKED = 2
-TINY = 2.0 ** -60
+RUN = 4
+FLOOR_LOGIT = -41.0
+AGAIN = (6, 7)
+REPEAT_AFTER = (0, 2)
+SIGMOID_ORDER = ((0, 1, 2, 3, 4, 5, 6, 7), (6, 7, 2, 0, 3, 1, 4, 5))
+MAXIMUM_ORDER = ((0, 1, 2, 3, 4, 5, 6, 7), (0, 1, 2, 3, 4, 6, 7, 5))
 
 
 def tile_list_claim_count_rates_kernel(
@@ -48,21 +52,22 @@ def tile_list_claim_count_rates_kernel(
 
         tab_rows = held([P, T // 4], I32, "tab_rows")
         nc.vector.memset(tab_rows[:], 0)
-        warm = held([P, 8], F32, "warm")
-        nc.vector.memset(warm[:, 0:1], 0.0)
-        nc.scalar.activation(warm[:, 4:5], warm[:, 0:1], ACT.Sigmoid)
+        floor = held([P, 16], F32, "floor")
+        nc.vector.memset(floor[:, 0:1], FLOOR_LOGIT)
+        nc.scalar.activation(floor[:, 8:9], floor[:, 0:1], ACT.Sigmoid)
 
-        w4_rows = held([P, PASSES, H // 4], I32, "w4_rows")
+        w4_rows = held([P, H // 4], I32, "w4_rows")
         tab2_rows = held([P, T2 // 4], I32, "tab2_rows")
-        v_scale = held([P, PASSES, S // 4], I32, "v_scale")
+        low_rows = held([P, 2, S // 4], I32, "low_rows")
 
         tab = [held([P, T], I32, "tab%d" % a) for a in range(PASSES)]
         v_words = [held([P, S], U32, "v_words%d" % a) for a in range(PASSES)]
+        v_scale = held([P, S], U8, "v_scale")
         w1_codes = held([P, PASSES, PASSES, PASS], U32, "w1_codes")
         w1_scale = held([P, PASSES, PASSES, PASS], U8, "w1_scale")
 
         def load_w1(a, b):
-            raw = keep.tile([P, PACK, PASS], F32, name="w1_raw", tag="shared%d" % a)
+            raw = held([P, PACK, PASS], F32, "w1_raw%d%d" % (a, b))
             rows = w1[a * PASS : (a + 1) * PASS, b * PASS : (b + 1) * PASS]
             nc.sync.dma_start(raw[:], rows.rearrange("(p j) c -> p j c", j=PACK))
             return raw
@@ -70,17 +75,24 @@ def tile_list_claim_count_rates_kernel(
         def load_tab(a):
             nc.sync.dma_start(tab[a][:], tab_words[a].rearrange("p t i -> p (t i)").bitcast(I32))
 
-        def round_w1(raw, grouped, copy):
-            copy(grouped.rearrange("p t m j -> p m t j"), raw[:].rearrange("p j (m t) -> p m t j", t=PACK))
+        def load_rows(rows, scales):
+            for q in range(4):
+                nc.sync.dma_start(rows[32 * q : 32 * q + 8, :], scales.bitcast(I32)[:, 4 * q : 4 * q + 4, :])
 
-        def quantize_w1(grouped, b):
-            nc.vector.quantize_mx(
-                out=w1_codes[:, b].rearrange("p a c -> p (a c)").bitcast(FP8X4),
-                scales=w1_scale[:, b].rearrange("p a c -> p (a c)"),
-                in_=grouped[:].rearrange("p a t m j -> p (a t m j)"),
+        w1_bf16 = [[held([P, PACK, P, PACK], BF16, "w1_bf16_%d%d" % (a, b)) for b in range(PASSES)] for a in range(PASSES)]
+
+        def round_w1(raw, a, b, copy, low=0, high=P):
+            copy(
+                w1_bf16[a][b][:, :, low:high, :].rearrange("p t m j -> p m t j"),
+                raw[:].rearrange("p j (m t) -> p m t j", t=PACK),
             )
 
-        w1_bf16 = [held([P, PASSES, PACK, P, PACK], BF16, "w1_bf16_%d" % b) for b in range(PASSES)]
+        def quantize_w1(a, b, low=0, high=PACK):
+            nc.vector.quantize_mx(
+                out=w1_codes[:, b, a, low * P : high * P].bitcast(FP8X4),
+                scales=w1_scale[:, b, a, low * P : high * P],
+                in_=w1_bf16[a][b][:, low:high].rearrange("p t m j -> p (t m j)"),
+            )
 
         def gather_v(a, half):
             nc.vector.tensor_copy(
@@ -88,58 +100,43 @@ def tile_list_claim_count_rates_kernel(
                 tab[a][:].bitcast(U32).indirect(holders[:, half * HALF // 16 : (half + 1) * HALF // 16]),
             )
 
-        picked_rows = held([P, S], U8, "picked_rows")
-
-        def move_rows(a):
-            for q in range(4):
-                first = 64 * a + 16 * q
-                nc.sync.dma_start(
-                    v_scale[32 * q : 32 * q + 4, a, :], picked_rows[first : first + 16 : 4, :].bitcast(I32)
-                )
-
-        raw00 = load_w1(0, 0)
         nc.sync.dma_start(holders[:], offs)
-        nc.sync.dma_start(tab_rows[0:P:4, :], tab_scales.rearrange("a q t -> (a q) t").bitcast(I32))
         load_tab(0)
-        raw10 = load_w1(1, 0)
-        nc.vector.memset(v_scale[:], 0)
-        nc.vector.tensor_copy(picked_rows[:], tab_rows[:].bitcast(U8).indirect(holders[:]))
-        move_rows(0)
+        load_rows(tab_rows, tab_scales)
+        raw00 = load_w1(0, 0)
+        nc.sync.dma_start(perils[:], offs2)
+        nc.vector.memset(tab2_rows[:], 0)
+        load_rows(tab2_rows, tab2_scales)
         load_tab(1)
-        move_rows(1)
+        raw10 = [held([P, PACK, QUARTER], F32, "w1_raw10_%d" % u) for u in range(2)]
+        for u in range(2):
+            rows = w1[PASS : 2 * PASS, u * QUARTER : (u + 1) * QUARTER]
+            nc.sync.dma_start(raw10[u][:], rows.rearrange("(p j) c -> p j c", j=PACK))
+        gather_v(0, 0)
+        nc.vector.tensor_copy(v_scale[:], tab_rows[:].bitcast(U8).indirect(holders[:]))
+        gather_v(0, 1)
+        v2_scale = held([P, S2], U8, "v2_scale")
+        nc.vector.tensor_copy(v2_scale[:], tab2_rows[:].bitcast(U8).indirect(perils[:]))
+        round_w1(raw00, 0, 0, nc.scalar.copy)
+        quantize_w1(0, 0)
+        gather_v(1, 0)
+        gather_v(1, 1)
+        round_w1(raw10[0], 1, 0, nc.scalar.copy, 0, P // 2)
+        round_w1(raw10[1], 1, 0, nc.vector.tensor_copy, P // 2, P)
+        quantize_w1(1, 0, 0, 1)
+        quantize_w1(1, 0, 1, 2)
+        quantize_w1(1, 0, 2, 4)
 
         w4_raw = held([P, PASSES, H // 2], I32, "w4_raw")
         nc.sync.dma_start(w4_raw[:], w4_words.bitcast(I32).rearrange("a p c -> p a c"))
-        round_w1(raw00, w1_bf16[0][:, 0], nc.scalar.copy)
-        raw01 = load_w1(0, 1)
         nc.vector.memset(w4_rows[:], 0)
-        for q in range(4):
-            nc.sync.dma_start(
-                w4_rows[32 * q : 32 * q + 4, :, :],
-                w4_scales.bitcast(I32)[:, 4 * q : 4 * q + 4, :].rearrange("a r c -> r a c"),
-            )
-        gather_v(0, 0)
-        gather_v(0, 1)
-        round_w1(raw10, w1_bf16[0][:, 1], nc.scalar.copy)
-        quantize_w1(w1_bf16[0], 0)
-        raw11 = load_w1(1, 1)
-        gather_v(1, 0)
-        gather_v(1, 1)
+        load_rows(w4_rows, w4_scales)
+        raw01 = load_w1(0, 1)
+        nc.vector.memset(low_rows[:], 0)
 
-        nc.sync.dma_start(perils[:], offs2)
-        tab2 = held([P, PASSES, T2], I32, "tab2")
-        nc.sync.dma_start(tab2[:], tab2_words.rearrange("a p t i -> p a (t i)").bitcast(I32))
-        nc.vector.memset(tab2_rows[:], 0)
-        for q in range(4):
-            nc.sync.dma_start(tab2_rows[32 * q : 32 * q + 8, :], tab2_scales.bitcast(I32)[:, 4 * q : 4 * q + 4, :])
-        bias = held([P, S2 // P], F32, "bias")
-        with nc.allow_non_contiguous_dma(reason="one bias value for each partition"):
-            nc.sync.dma_start(bias[:], pb.rearrange("(i p) -> p i", p=P))
-        exposure = held([P, S], F32, "exposure")
-        nc.sync.dma_start(exposure[:], ex.partition_broadcast(P))
-
-        w4_codes = held([P, PASSES, PASSES, PACK, 2 * P], U8, "w4_codes")
-        w4_scale = held([P, PASSES, PASSES, PACK, P], U8, "w4_scale")
+        def lower_rows(which, packed):
+            for q in range(4):
+                nc.sync.dma_start(low_rows[32 * q : 32 * q + 4, which, :], packed[32 * q + 4 : 32 * q + 8, :].bitcast(I32))
 
         def permute(dst, src, run):
             nc.vector.tensor_copy(
@@ -147,91 +144,87 @@ def tile_list_claim_count_rates_kernel(
                 src.rearrange("p (g m i t) -> p g m t i", t=PACK, m=P // run, i=run),
             )
 
-        def permute_w4_codes():
-            permute(
-                w4_codes[:].rearrange("p a b t c -> p (a b t c)").bitcast(U16),
-                w4_raw[:].rearrange("p a c -> p (a c)").bitcast(U16),
-                8,
-            )
+        lower_rows(0, v_scale)
+        raw11 = load_w1(1, 1)
+        w4_scale = held([P, H], U8, "w4_scale")
+        permute(w4_scale[:], w4_rows[:].bitcast(U8), 16)
+        lower_rows(1, w4_scale)
+        tab2 = [held([P, T2], I32, "reused%d" % c) for c in range(PASSES)]
+        for c in range(PASSES):
+            nc.sync.dma_start(tab2[c][:], tab2_words[c].rearrange("p t i -> p (t i)").bitcast(I32))
+        bias = held([P, S2 // P], F32, "bias")
+        with nc.allow_non_contiguous_dma(reason="one bias value for each partition"):
+            nc.sync.dma_start(bias[:], pb.rearrange("(i p) -> p i", p=P))
+        exposure = held([P, S], F32, "exposure")
+        nc.sync.dma_start(exposure[:], ex.partition_broadcast(P))
 
-        def permute_w4_scales():
-            permute(
-                w4_scale[:].rearrange("p a b t m -> p (a b t m)"),
-                w4_rows[:].rearrange("p a c -> p (a c)").bitcast(U8),
-                16,
-            )
-
-        v_planes = [v_scale[:, a, :].bitcast(U8) for a in range(PASSES)]
-
-        def product(dst, codes, scale, first, width):
-            for a in range(PASSES):
-                nc.tensor.matmul_mx(
-                    out=dst,
-                    lhsT=codes(a),
-                    lhsT_scale=scale(a),
-                    rhs=v_words[a][:, first : first + width].bitcast(FP8X4),
-                    rhs_scale=v_planes[a][:, first : first + width],
-                    start=(a == 0),
-                    stop=(a == PASSES - 1),
-                )
+        w4_codes = held([P, PASSES, PASSES, PACK, 2 * P], U8, "w4_codes")
 
         h_codes = held([P, PASSES, S], U32, "h_codes")
         h_scale = held([P, PASSES, S], U8, "h_scale")
         v2_words = held([P, PASSES, S2], U32, "v2_words")
-        v2_scale = held([P, S2], U8, "v2_scale")
-        gate = [held([P, BANKS, HALF + SLIVER], F32, "gate%d" % b) for b in range(PASSES)]
+        gate = held([P, BANKS, HALF + SLIVER], F32, "gate")
         h = [held([P, S, PACK], BF16, "h%d" % b) for b in range(PASSES)]
 
+        def shaped(b, k, flat):
+            return flat.rearrange("p (g n) -> p g n", g=BANKS) if k == SIGMOID_ORDER[b][-1] else flat
+
         def gate_of(b, k):
-            if k < BANKS - 1:
-                return gate[b][:, k, 0:HALF].rearrange("p (g n e) -> p g n e", g=BANKS, e=2)
-            return gate[b][:, :, HALF:].rearrange("p g (n e) -> p g n e", e=2)
+            return gate[:, :, HALF:] if k == SIGMOID_ORDER[b][-1] else gate[:, SIGMOID_ORDER[b].index(k), 0:HALF]
 
-        def logits(b, k):
-            jq, u = divmod(k, 2)
-            z = bank((k - b * PARKED) % BANKS, [P, 2, QUARTER])
-            for e in range(2):
-                t = 2 * u + e
-                cols = slice(t * P, (t + 1) * P)
-                product(
-                    z[:, e, :],
-                    lambda a: w1_codes[:, b, a, cols].bitcast(FP8X4),
-                    lambda a: w1_scale[:, b, a, cols],
-                    jq * QUARTER,
-                    QUARTER,
-                )
-            z_view = z[:].rearrange("p e (g n) -> p g n e", g=BANKS)
-            nc.scalar.activation(gate_of(b, k), z_view, ACT.Sigmoid, scale=-1.0)
-            return z_view
-
-        def logs(b):
-            for k in range(BANKS):
-                part = gate[b][:, k, :] if k < BANKS - 1 else gate[b][:, k, HALF:]
-                nc.scalar.activation(part, part, ACT.Ln, bias=TINY)
-
-        def softplus(b, k, z_view):
-            nc.vector.scalar_tensor_tensor(
-                soft[:, k].rearrange("p (g n) e -> p g n e", g=BANKS), gate_of(b, k), -1.0, z_view, ALU.mult, ALU.max
+        def logit_pass(z, b, k, a):
+            half, t = divmod(k, PACK)
+            cols = slice(t * P, (t + 1) * P)
+            picked = slice(half * HALF, (half + 1) * HALF)
+            nc.tensor.matmul_mx(
+                out=z[:],
+                lhsT=w1_codes[:, b, a, cols].bitcast(FP8X4),
+                lhsT_scale=w1_scale[:, b, a, cols],
+                rhs=v_words[a][:, picked].bitcast(FP8X4),
+                rhs_scale=v_scale[4 * a :, picked],
+                start=(a == 0),
+                stop=(a == PASSES - 1),
             )
 
-        def linear(b, j):
-            lin = bank((j - PARKED) % BANKS, [P, PACK, BLOCK])
+        def sigmoid(b, k, z):
+            nc.scalar.activation(gate_of(b, k), shaped(b, k, z[:]), ACT.Sigmoid, scale=-1.0)
+
+        def logs(b):
+            for k in MAXIMUM_ORDER[b]:
+                row = SIGMOID_ORDER[b].index(k)
+                part = gate[:, row, HALF:] if row == BANKS - 1 else gate[:, row, :]
+                nc.scalar.activation(part, part, ACT.Ln, bias=floor[:, 8:9])
+
+        def softplus(b, k, z):
+            nc.vector.scalar_tensor_tensor(
+                shaped(b, k, soft[:, k // PACK, k % PACK]), gate_of(b, k), -1.0, shaped(b, k, z[:]), ALU.mult, ALU.max
+            )
+
+        v_planes = [v_scale[:], low_rows[:, 0, :].bitcast(U8)]
+        w4_planes = [w4_scale[:], low_rows[:, 1, :].bitcast(U8)]
+
+        def linear(b, j, k):
+            lin = bank(k, [P, PACK, BLOCK])
+            picked = slice(j * BLOCK, (j + 1) * BLOCK)
             for t in range(PACK):
-                product(
-                    lin[:, t, :],
-                    lambda a: w4_codes[:, a, b, t, :].bitcast(FP4X4),
-                    lambda a: w4_scale[:, a, b, t, :],
-                    j * BLOCK,
-                    BLOCK,
-                )
+                for a in range(PASSES):
+                    nc.tensor.matmul_mx(
+                        out=lin[:, t, :],
+                        lhsT=w4_codes[:, a, b, t, :].bitcast(FP4X4),
+                        lhsT_scale=w4_planes[a][:, b * PASS + t * P : b * PASS + (t + 1) * P],
+                        rhs=v_words[a][:, picked].bitcast(FP8X4),
+                        rhs_scale=v_planes[a][:, picked],
+                        start=(a == 0),
+                        stop=(a == PASSES - 1),
+                    )
             return lin
 
         def gated(b, j, lin):
-            jq, half = divmod(j, 2)
+            half, jj = divmod(j, PACK)
             nc.vector.tensor_tensor(
-                h[b][:, j * BLOCK : (j + 1) * BLOCK, :].rearrange("p n (u e) -> p n u e", e=2),
-                lin[:].rearrange("p (u e) n -> p n u e", e=2),
-                soft[:, 2 * jq : 2 * jq + 2, half * BLOCK : (half + 1) * BLOCK, :].rearrange("p u n e -> p n u e"),
+                h[b][:, j * BLOCK : (j + 1) * BLOCK, :].rearrange("p (c i) t -> p c t i", i=RUN),
+                lin[:].rearrange("p t (c i) -> p c t i", i=RUN),
+                soft[:, half, :, jj * BLOCK : (jj + 1) * BLOCK].rearrange("p t (c i) -> p c t i", i=RUN),
                 ALU.mult,
             )
 
@@ -242,12 +235,12 @@ def tile_list_claim_count_rates_kernel(
                 in_=h[b][:, first : first + width, :].rearrange("p n t -> p (n t)"),
             )
 
-        def rates(first, width):
+        def rates(first, width, banks):
             cols = slice(first, first + width)
-            tiles_in_bank = HALF // width
+            tiles_in_bank = PACK // len(banks)
             counts = held([P, PACK, width], F32, "counts%d" % first)
-            for group in range(PACK // tiles_in_bank):
-                y = bank((first // BLOCK + group - PARKED) % BANKS, [P, tiles_in_bank, width])
+            for group, k in enumerate(banks):
+                y = bank(k, [P, tiles_in_bank, width])
                 for e in range(tiles_in_bank):
                     i = tiles_in_bank * group + e
                     for b in range(PASSES):
@@ -277,61 +270,123 @@ def tile_list_claim_count_rates_kernel(
                         counts[:, low : low + stored, :],
                     )
 
-        z_views = [logits(0, k) for k in range(BANKS - 1)]
-        parked = held([P, BANKS, SLIVER // 2, 2], F32, "parked")
-        nc.scalar.copy(parked[:], z_views[BANKS - 2])
-        z_views[BANKS - 2] = parked[:]
-        z_views.append(logits(0, BANKS - 1))
-        permute_w4_codes()
-        round_w1(raw01, w1_bf16[1][:, 0], nc.vector.tensor_copy)
-        round_w1(raw11, w1_bf16[1][:, 1], nc.vector.tensor_copy)
-        permute_w4_scales()
-        soft = keep.tile([P, BANKS, QUARTER, 2], F32, name="soft", tag="shared1")
-        last = soft[:, BANKS - 1].rearrange("p (g n) e -> p g n e", g=BANKS)
-        nc.vector.tensor_copy(last, z_views[BANKS - 1])
-        z_views[BANKS - 1] = last
-        quantize_w1(w1_bf16[1], 1)
-
-        logs(0)
-        lins = [linear(0, j) for j in range(PARKED)]
+        zs = [bank(k, [P, HALF]) for k in range(BANKS)]
         for k in range(BANKS):
-            softplus(0, k, z_views[k])
-            if k + PARKED < BANKS:
-                lins.append(linear(0, k + PARKED))
-        z_views = []
-        for j in range(BANKS):
-            gated(0, j, lins[j])
-            z_views.append(logits(1, j))
+            logit_pass(zs[k], 0, k, 0)
+        for k in range(BANKS):
+            logit_pass(zs[k], 0, k, 1)
+            sigmoid(0, k, zs[k])
+        permute(
+            w4_codes[:].rearrange("p a b t c -> p (a b t c)").bitcast(U16),
+            w4_raw[:].rearrange("p a c -> p (a c)").bitcast(U16),
+            8,
+        )
+
+        def gather_v2(c):
+            nc.vector.tensor_copy(v2_words[:, c, :], tab2[c][:].bitcast(U32).indirect(perils[:]))
+
+        round_w1(raw01, 0, 1, nc.vector.tensor_copy)
+        round_w1(raw11, 1, 1, nc.vector.tensor_copy)
+        quantize_w1(0, 1)
+        quantize_w1(1, 1)
+        gather_v2(0)
+        soft = held([P, PASSES, PACK, HALF], F32, "reused0")
+
+        def logits(b, unit, k):
+            z = bank(k, [P, HALF])
+            for a in range(PASSES):
+                logit_pass(z, b, unit, a)
+            return z
+
+        def maximum(b, n):
+            k = MAXIMUM_ORDER[b][n]
+            softplus(b, k, zs[k])
+            again = n - REPEAT_AFTER[b]
+            if 0 <= again < len(AGAIN):
+                z_bank[AGAIN[again]] = z_bank[k]
+                zs[AGAIN[again]] = logits(b, AGAIN[again], z_bank[k])
+            else:
+                lin_bank.append(z_bank[k])
+                lins.append(linear(b, len(lins), z_bank[k]))
+
+        z_bank = list(range(BANKS))
+        lin_bank = list(AGAIN)
+        lins = [linear(0, j, k) for j, k in enumerate(lin_bank)]
+        logs(0)
+        following = {}
+
+        def next_logits(k, place):
+            following[k] = (logits(1, k, place), place)
+            sigmoid(1, k, following[k][0])
+
+        for n in range(5):
+            maximum(0, n)
+        gated(0, 0, lins[0])
+        next_logits(6, lin_bank[0])
+        maximum(0, 5)
+        gated(0, 1, lins[1])
+        next_logits(7, lin_bank[1])
+        maximum(0, 6)
+        maximum(0, 7)
+        gated(0, 2, lins[2])
+        next_logits(2, lin_bank[2])
+        next_logits(0, lin_bank[0])
+        gated(0, 3, lins[3])
+        next_logits(3, lin_bank[3])
+        next_logits(1, lin_bank[1])
+        gated(0, 4, lins[4])
+        next_logits(4, lin_bank[4])
+        gated(0, 5, lins[5])
+        next_logits(5, lin_bank[5])
+        gated(0, 6, lins[6])
+        gated(0, 7, lins[7])
         for half in range(2):
             quantize_h(0, half * HALF, HALF)
-        for c in range(PASSES):
-            nc.vector.tensor_copy(v2_words[:, c, :], tab2[:, c, :].bitcast(U32).indirect(perils[:]))
-        nc.vector.tensor_copy(v2_scale[:], tab2_rows[:].bitcast(U8).indirect(perils[:]))
+        gather_v2(1)
+        soft = held([P, PASSES, PACK, HALF], F32, "reused1")
 
+        zs = [following[k][0] for k in range(BANKS)]
+        z_bank = [following[k][1] for k in range(BANKS)]
+        lin_bank = lin_bank[6:]
+        lins = [linear(1, j, k) for j, k in enumerate(lin_bank)]
         logs(1)
-        lins = []
-        pieces = [(0, QUARTER), (QUARTER, QUARTER), (2 * QUARTER, QUARTER), (6 * BLOCK, BLOCK), (7 * BLOCK, BLOCK)]
+        pieces = [
+            (0, QUARTER, (0, 1)),
+            (QUARTER, QUARTER, (2, 3)),
+            (4 * BLOCK, BLOCK, (0,)),
+            (5 * BLOCK, BLOCK, (1,)),
+            (6 * BLOCK, BLOCK, (4, 5)),
+            (7 * BLOCK, BLOCK, (2, 3, 6, 7)),
+        ]
         done = []
 
         def finish(piece):
-            quantize_h(1, *pieces[piece])
-            done.append(rates(*pieces[piece]))
+            first, width, freed = pieces[piece]
+            quantize_h(1, first, width)
+            done.append(rates(first, width, [lin_bank[j] for j in freed]))
 
-        for step in range(BANKS):
-            softplus(1, step, z_views[step])
-            lins.append(linear(1, step))
-            if step in (4, 6):
-                finish(step // 2 - 2)
-            if step >= 2:
-                gated(1, step - 2, lins[step - 2])
-        gated(1, 6, lins[6])
+        for n in range(5):
+            maximum(1, n)
+        gated(1, 0, lins[0])
+        gated(1, 1, lins[1])
+        gated(1, 2, lins[2])
+        finish(0)
+        gated(1, 3, lins[3])
+        maximum(1, 5)
+        finish(1)
+        maximum(1, 6)
+        maximum(1, 7)
+        gated(1, 4, lins[4])
+        gated(1, 5, lins[5])
         finish(2)
-        gated(1, 7, lins[7])
+        gated(1, 6, lins[6])
         finish(3)
         finish(4)
-        expose(*pieces[0], done[0], nc.gpsimd, 1, 2, nc.sync)
-        expose(*pieces[1], done[1], nc.gpsimd, 1, 2, nc.sync, 0, 2)
-        expose(*pieces[1], done[1], nc.vector, 2, 2, nc.sync, 2, 4)
-        expose(*pieces[2], done[2], nc.vector, 2, 2, nc.scalar)
-        expose(*pieces[3], done[3], nc.vector, 4, 4, nc.scalar)
-        expose(*pieces[4], done[4], nc.vector, 2, 2, nc.scalar)
+        gated(1, 7, lins[7])
+        finish(5)
+        expose(*pieces[0][:2], done[0], nc.gpsimd, 2, 2, nc.sync)
+        expose(*pieces[1][:2], done[1], nc.gpsimd, 2, 2, nc.sync)
+        expose(*pieces[2][:2], done[2], nc.vector, 4, 4, nc.scalar)
+        expose(*pieces[3][:2], done[3], nc.vector, 4, 4, nc.scalar)
+        expose(*pieces[4][:2], done[4], nc.vector, 4, 4, nc.scalar)
+        expose(*pieces[5][:2], done[5], nc.vector, 2, 2, nc.scalar)

@@ -25,12 +25,11 @@ QUARTER = 256
 BLOCK = 128
 HALF = 512
 SLIVER = 64
-RUN = 4
 FLOOR_LOGIT = -41.0
-AGAIN = (6, 7)
+SCALAR_SHARE = 40
+AGAIN = ((6, 7), (4, 5))
 REPEAT_AFTER = (0, 2)
-SIGMOID_ORDER = ((0, 1, 2, 3, 4, 5, 6, 7), (6, 7, 2, 0, 3, 1, 4, 5))
-MAXIMUM_ORDER = ((0, 1, 2, 3, 4, 5, 6, 7), (0, 1, 2, 3, 4, 6, 7, 5))
+SIGMOID_ORDER = ((0, 1, 2, 3, 4, 5, 6, 7), (4, 5, 2, 0, 3, 1, 6, 7))
 
 
 def tile_list_claim_count_rates_kernel(
@@ -58,11 +57,12 @@ def tile_list_claim_count_rates_kernel(
 
         w4_rows = held([P, H // 4], I32, "w4_rows")
         tab2_rows = held([P, T2 // 4], I32, "tab2_rows")
-        low_rows = held([P, 2, S // 4], I32, "low_rows")
+        w4_low = held([P, H // 4], I32, "w4_low")
+        v_scale = held([P, PASSES, S // 4], I32, "v_scale")
+        v2_scale = held([P, S2 // 4], I32, "v2_scale")
 
         tab = [held([P, T], I32, "tab%d" % a) for a in range(PASSES)]
         v_words = [held([P, S], U32, "v_words%d" % a) for a in range(PASSES)]
-        v_scale = held([P, S], U8, "v_scale")
         w1_codes = held([P, PASSES, PASSES, PASS], U32, "w1_codes")
         w1_scale = held([P, PASSES, PASSES, PASS], U8, "w1_scale")
 
@@ -84,7 +84,7 @@ def tile_list_claim_count_rates_kernel(
         def round_w1(raw, a, b, copy, low=0, high=P):
             copy(
                 w1_bf16[a][b][:, :, low:high, :].rearrange("p t m j -> p m t j"),
-                raw[:].rearrange("p j (m t) -> p m t j", t=PACK),
+                raw[:].rearrange("p j (m t) -> p m t j", t=PACK)[:, low:high],
             )
 
         def quantize_w1(a, b, low=0, high=PACK):
@@ -100,31 +100,40 @@ def tile_list_claim_count_rates_kernel(
                 tab[a][:].bitcast(U32).indirect(holders[:, half * HALF // 16 : (half + 1) * HALF // 16]),
             )
 
-        nc.sync.dma_start(holders[:], offs)
-        load_tab(0)
-        load_rows(tab_rows, tab_scales)
+        def spread_rows(rows, scales):
+            nc.sync.dma_start(rows[0:P:4, :], scales.rearrange("a q t -> (a q) t").bitcast(I32))
+
+        def place_rows(dst, low, picked, a):
+            for q in range(4):
+                first = 64 * a + 16 * q
+                nc.sync.dma_start(dst[32 * q + low : 32 * q + low + 4, :], picked[first : first + 16 : 4, :].bitcast(I32))
+
+        picked_rows = held([P, S], U8, "picked_rows")
+        picked2_rows = held([P, S2], U8, "picked2_rows")
+
         raw00 = load_w1(0, 0)
+        nc.sync.dma_start(holders[:], offs)
+        spread_rows(tab_rows, tab_scales)
         nc.sync.dma_start(perils[:], offs2)
         nc.vector.memset(tab2_rows[:], 0)
-        load_rows(tab2_rows, tab2_scales)
+        spread_rows(tab2_rows, tab2_scales)
+        load_tab(0)
         load_tab(1)
-        raw10 = [held([P, PACK, QUARTER], F32, "w1_raw10_%d" % u) for u in range(2)]
-        for u in range(2):
-            rows = w1[PASS : 2 * PASS, u * QUARTER : (u + 1) * QUARTER]
-            nc.sync.dma_start(raw10[u][:], rows.rearrange("(p j) c -> p j c", j=PACK))
-        gather_v(0, 0)
-        nc.vector.tensor_copy(v_scale[:], tab_rows[:].bitcast(U8).indirect(holders[:]))
-        gather_v(0, 1)
-        v2_scale = held([P, S2], U8, "v2_scale")
-        nc.vector.tensor_copy(v2_scale[:], tab2_rows[:].bitcast(U8).indirect(perils[:]))
+        nc.vector.memset(v_scale[:], 0)
+        nc.vector.tensor_copy(picked_rows[:], tab_rows[:].bitcast(U8).indirect(holders[:]))
+        place_rows(v_scale[:, 0, :], 0, picked_rows, 0)
+        raw10 = load_w1(1, 0)
+        place_rows(v_scale[:, 1, :], 0, picked_rows, 1)
+        nc.vector.tensor_copy(picked2_rows[:], tab2_rows[:].bitcast(U8).indirect(perils[:]))
         round_w1(raw00, 0, 0, nc.scalar.copy)
         quantize_w1(0, 0)
+        gather_v(0, 0)
+        gather_v(0, 1)
         gather_v(1, 0)
         gather_v(1, 1)
-        round_w1(raw10[0], 1, 0, nc.scalar.copy, 0, P // 2)
-        round_w1(raw10[1], 1, 0, nc.vector.tensor_copy, P // 2, P)
-        quantize_w1(1, 0, 0, 1)
-        quantize_w1(1, 0, 1, 2)
+        round_w1(raw10, 1, 0, nc.scalar.copy, 0, SCALAR_SHARE)
+        round_w1(raw10, 1, 0, nc.vector.tensor_copy, SCALAR_SHARE, P)
+        quantize_w1(1, 0, 0, 2)
         quantize_w1(1, 0, 2, 4)
 
         w4_raw = held([P, PASSES, H // 2], I32, "w4_raw")
@@ -132,11 +141,7 @@ def tile_list_claim_count_rates_kernel(
         nc.vector.memset(w4_rows[:], 0)
         load_rows(w4_rows, w4_scales)
         raw01 = load_w1(0, 1)
-        nc.vector.memset(low_rows[:], 0)
-
-        def lower_rows(which, packed):
-            for q in range(4):
-                nc.sync.dma_start(low_rows[32 * q : 32 * q + 4, which, :], packed[32 * q + 4 : 32 * q + 8, :].bitcast(I32))
+        nc.vector.memset(w4_low[:], 0)
 
         def permute(dst, src, run):
             nc.vector.tensor_copy(
@@ -144,11 +149,11 @@ def tile_list_claim_count_rates_kernel(
                 src.rearrange("p (g m i t) -> p g m t i", t=PACK, m=P // run, i=run),
             )
 
-        lower_rows(0, v_scale)
         raw11 = load_w1(1, 1)
         w4_scale = held([P, H], U8, "w4_scale")
         permute(w4_scale[:], w4_rows[:].bitcast(U8), 16)
-        lower_rows(1, w4_scale)
+        for q in range(4):
+            nc.sync.dma_start(w4_low[32 * q : 32 * q + 4, :], w4_scale[32 * q + 4 : 32 * q + 8, :].bitcast(I32))
         tab2 = [held([P, T2], I32, "reused%d" % c) for c in range(PASSES)]
         for c in range(PASSES):
             nc.sync.dma_start(tab2[c][:], tab2_words[c].rearrange("p t i -> p (t i)").bitcast(I32))
@@ -157,6 +162,9 @@ def tile_list_claim_count_rates_kernel(
             nc.sync.dma_start(bias[:], pb.rearrange("(i p) -> p i", p=P))
         exposure = held([P, S], F32, "exposure")
         nc.sync.dma_start(exposure[:], ex.partition_broadcast(P))
+        nc.vector.memset(v2_scale[:], 0)
+        for a in range(PASSES):
+            place_rows(v2_scale, 4 * a, picked2_rows, a)
 
         w4_codes = held([P, PASSES, PASSES, PACK, 2 * P], U8, "w4_codes")
 
@@ -166,42 +174,46 @@ def tile_list_claim_count_rates_kernel(
         gate = held([P, BANKS, HALF + SLIVER], F32, "gate")
         h = [held([P, S, PACK], BF16, "h%d" % b) for b in range(PASSES)]
 
-        def shaped(b, k, flat):
-            return flat.rearrange("p (g n) -> p g n", g=BANKS) if k == SIGMOID_ORDER[b][-1] else flat
+        v_planes = [v_scale[:, a, :].bitcast(U8) for a in range(PASSES)]
 
         def gate_of(b, k):
-            return gate[:, :, HALF:] if k == SIGMOID_ORDER[b][-1] else gate[:, SIGMOID_ORDER[b].index(k), 0:HALF]
+            if k == SIGMOID_ORDER[b][-1]:
+                return gate[:, :, HALF:].rearrange("p g (n e) -> p g n e", e=2)
+            return gate[:, SIGMOID_ORDER[b].index(k), 0:HALF].rearrange("p (g n e) -> p g n e", g=BANKS, e=2)
+
+        def paired(z):
+            return z[:].rearrange("p e (g n) -> p g n e", g=BANKS)
 
         def logit_pass(z, b, k, a):
-            half, t = divmod(k, PACK)
-            cols = slice(t * P, (t + 1) * P)
-            picked = slice(half * HALF, (half + 1) * HALF)
-            nc.tensor.matmul_mx(
-                out=z[:],
-                lhsT=w1_codes[:, b, a, cols].bitcast(FP8X4),
-                lhsT_scale=w1_scale[:, b, a, cols],
-                rhs=v_words[a][:, picked].bitcast(FP8X4),
-                rhs_scale=v_scale[4 * a :, picked],
-                start=(a == 0),
-                stop=(a == PASSES - 1),
-            )
+            quarter, u = divmod(k, 2)
+            picked = slice(quarter * QUARTER, (quarter + 1) * QUARTER)
+            for e in range(2):
+                cols = slice((2 * u + e) * P, (2 * u + e + 1) * P)
+                nc.tensor.matmul_mx(
+                    out=z[:, e, :],
+                    lhsT=w1_codes[:, b, a, cols].bitcast(FP8X4),
+                    lhsT_scale=w1_scale[:, b, a, cols],
+                    rhs=v_words[a][:, picked].bitcast(FP8X4),
+                    rhs_scale=v_planes[a][:, picked],
+                    start=(a == 0 and e == 0),
+                    stop=(a == PASSES - 1 and e == 1),
+                )
 
         def sigmoid(b, k, z):
-            nc.scalar.activation(gate_of(b, k), shaped(b, k, z[:]), ACT.Sigmoid, scale=-1.0)
+            nc.scalar.activation(gate_of(b, k), paired(z), ACT.Sigmoid, scale=-1.0)
 
         def logs(b):
-            for k in MAXIMUM_ORDER[b]:
+            for k in range(BANKS):
                 row = SIGMOID_ORDER[b].index(k)
                 part = gate[:, row, HALF:] if row == BANKS - 1 else gate[:, row, :]
                 nc.scalar.activation(part, part, ACT.Ln, bias=floor[:, 8:9])
 
         def softplus(b, k, z):
             nc.vector.scalar_tensor_tensor(
-                shaped(b, k, soft[:, k // PACK, k % PACK]), gate_of(b, k), -1.0, shaped(b, k, z[:]), ALU.mult, ALU.max
+                soft[:, k].rearrange("p (g n) e -> p g n e", g=BANKS), gate_of(b, k), -1.0, paired(z), ALU.mult, ALU.max
             )
 
-        v_planes = [v_scale[:], low_rows[:, 0, :].bitcast(U8)]
-        w4_planes = [w4_scale[:], low_rows[:, 1, :].bitcast(U8)]
+        w4_planes = [w4_scale[:], w4_low[:].bitcast(U8)]
 
         def linear(b, j, k):
             lin = bank(k, [P, PACK, BLOCK])
@@ -220,11 +232,11 @@ def tile_list_claim_count_rates_kernel(
             return lin
 
         def gated(b, j, lin):
-            half, jj = divmod(j, PACK)
+            quarter, half = divmod(j, 2)
             nc.vector.tensor_tensor(
-                h[b][:, j * BLOCK : (j + 1) * BLOCK, :].rearrange("p (c i) t -> p c t i", i=RUN),
-                lin[:].rearrange("p t (c i) -> p c t i", i=RUN),
-                soft[:, half, :, jj * BLOCK : (jj + 1) * BLOCK].rearrange("p t (c i) -> p c t i", i=RUN),
+                h[b][:, j * BLOCK : (j + 1) * BLOCK, :].rearrange("p n (u e) -> p n u e", e=2),
+                lin[:].rearrange("p (u e) n -> p n u e", e=2),
+                soft[:, 2 * quarter : 2 * quarter + 2, half * BLOCK : (half + 1) * BLOCK, :].rearrange("p u n e -> p n u e"),
                 ALU.mult,
             )
 
@@ -247,7 +259,7 @@ def tile_list_claim_count_rates_kernel(
                         nc.tensor.matmul_mx(
                             out=y[:, e, :],
                             lhsT=v2_words[:, b, i * P : (i + 1) * P].bitcast(FP8X4),
-                            lhsT_scale=v2_scale[4 * b :, i * P : (i + 1) * P],
+                            lhsT_scale=v2_scale[:].bitcast(U8)[4 * b :, i * P : (i + 1) * P],
                             rhs=h_codes[:, b, cols].bitcast(FP8X4),
                             rhs_scale=h_scale[:, b, cols],
                             start=(b == 0),
@@ -270,7 +282,7 @@ def tile_list_claim_count_rates_kernel(
                         counts[:, low : low + stored, :],
                     )
 
-        zs = [bank(k, [P, HALF]) for k in range(BANKS)]
+        zs = [bank(k, [P, 2, QUARTER]) for k in range(BANKS)]
         for k in range(BANKS):
             logit_pass(zs[k], 0, k, 0)
         for k in range(BANKS):
@@ -290,27 +302,27 @@ def tile_list_claim_count_rates_kernel(
         quantize_w1(0, 1)
         quantize_w1(1, 1)
         gather_v2(0)
-        soft = held([P, PASSES, PACK, HALF], F32, "reused0")
+        soft = held([P, BANKS, QUARTER, 2], F32, "reused0")
 
         def logits(b, unit, k):
-            z = bank(k, [P, HALF])
+            z = bank(k, [P, 2, QUARTER])
             for a in range(PASSES):
                 logit_pass(z, b, unit, a)
             return z
 
-        def maximum(b, n):
-            k = MAXIMUM_ORDER[b][n]
+        def maximum(b, k):
             softplus(b, k, zs[k])
-            again = n - REPEAT_AFTER[b]
-            if 0 <= again < len(AGAIN):
-                z_bank[AGAIN[again]] = z_bank[k]
-                zs[AGAIN[again]] = logits(b, AGAIN[again], z_bank[k])
+            again = k - REPEAT_AFTER[b]
+            if 0 <= again < len(AGAIN[b]):
+                repeated = AGAIN[b][again]
+                z_bank[repeated] = z_bank[k]
+                zs[repeated] = logits(b, repeated, z_bank[k])
             else:
                 lin_bank.append(z_bank[k])
                 lins.append(linear(b, len(lins), z_bank[k]))
 
         z_bank = list(range(BANKS))
-        lin_bank = list(AGAIN)
+        lin_bank = list(AGAIN[0])
         lins = [linear(0, j, k) for j, k in enumerate(lin_bank)]
         logs(0)
         following = {}
@@ -322,10 +334,10 @@ def tile_list_claim_count_rates_kernel(
         for n in range(5):
             maximum(0, n)
         gated(0, 0, lins[0])
-        next_logits(6, lin_bank[0])
+        next_logits(4, lin_bank[0])
         maximum(0, 5)
         gated(0, 1, lins[1])
-        next_logits(7, lin_bank[1])
+        next_logits(5, lin_bank[1])
         maximum(0, 6)
         maximum(0, 7)
         gated(0, 2, lins[2])
@@ -335,15 +347,15 @@ def tile_list_claim_count_rates_kernel(
         next_logits(3, lin_bank[3])
         next_logits(1, lin_bank[1])
         gated(0, 4, lins[4])
-        next_logits(4, lin_bank[4])
+        next_logits(6, lin_bank[4])
         gated(0, 5, lins[5])
-        next_logits(5, lin_bank[5])
+        next_logits(7, lin_bank[5])
         gated(0, 6, lins[6])
         gated(0, 7, lins[7])
         for half in range(2):
             quantize_h(0, half * HALF, HALF)
         gather_v2(1)
-        soft = held([P, PASSES, PACK, HALF], F32, "reused1")
+        soft = held([P, BANKS, QUARTER, 2], F32, "reused1")
 
         zs = [following[k][0] for k in range(BANKS)]
         z_bank = [following[k][1] for k in range(BANKS)]
@@ -353,9 +365,8 @@ def tile_list_claim_count_rates_kernel(
         pieces = [
             (0, QUARTER, (0, 1)),
             (QUARTER, QUARTER, (2, 3)),
-            (4 * BLOCK, BLOCK, (0,)),
-            (5 * BLOCK, BLOCK, (1,)),
-            (6 * BLOCK, BLOCK, (4, 5)),
+            (2 * QUARTER, QUARTER, (4, 5)),
+            (6 * BLOCK, BLOCK, (0, 1)),
             (7 * BLOCK, BLOCK, (2, 3, 6, 7)),
         ]
         done = []
@@ -365,28 +376,29 @@ def tile_list_claim_count_rates_kernel(
             quantize_h(1, first, width)
             done.append(rates(first, width, [lin_bank[j] for j in freed]))
 
-        for n in range(5):
-            maximum(1, n)
+        for k in range(3):
+            maximum(1, k)
         gated(1, 0, lins[0])
         gated(1, 1, lins[1])
-        gated(1, 2, lins[2])
+        maximum(1, 3)
         finish(0)
+        gated(1, 2, lins[2])
         gated(1, 3, lins[3])
-        maximum(1, 5)
+        maximum(1, 4)
         finish(1)
+        maximum(1, 5)
         maximum(1, 6)
         maximum(1, 7)
         gated(1, 4, lins[4])
         gated(1, 5, lins[5])
-        finish(2)
         gated(1, 6, lins[6])
+        finish(2)
         finish(3)
-        finish(4)
         gated(1, 7, lins[7])
-        finish(5)
-        expose(*pieces[0][:2], done[0], nc.gpsimd, 2, 2, nc.sync)
-        expose(*pieces[1][:2], done[1], nc.gpsimd, 2, 2, nc.sync)
-        expose(*pieces[2][:2], done[2], nc.vector, 4, 4, nc.scalar)
+        finish(4)
+        expose(*pieces[0][:2], done[0], nc.gpsimd, 1, 2, nc.sync)
+        expose(*pieces[1][:2], done[1], nc.gpsimd, 1, 2, nc.sync, 0, 2)
+        expose(*pieces[1][:2], done[1], nc.vector, 2, 2, nc.sync, 2, 4)
+        expose(*pieces[2][:2], done[2], nc.vector, 2, 2, nc.scalar)
         expose(*pieces[3][:2], done[3], nc.vector, 4, 4, nc.scalar)
-        expose(*pieces[4][:2], done[4], nc.vector, 4, 4, nc.scalar)
-        expose(*pieces[5][:2], done[5], nc.vector, 2, 2, nc.scalar)
+        expose(*pieces[4][:2], done[4], nc.vector, 2, 2, nc.scalar)

@@ -29,7 +29,7 @@ FLOOR_LOGIT = -41.0
 SCALAR_SHARE = 40
 AGAIN = ((6, 7), (4, 5))
 REPEAT_AFTER = (0, 2)
-SIGMOID_ORDER = ((0, 1, 2, 3, 4, 5, 6, 7), (4, 5, 2, 0, 3, 1, 6, 7))
+SIGMOID_ORDER = ((0, 1, 2, 3, 4, 5, 6, 7), (4, 5, 2, 0, 1, 3, 6, 7))
 
 
 def tile_list_claim_count_rates_kernel(
@@ -339,13 +339,13 @@ def tile_list_claim_count_rates_kernel(
         gated(0, 1, lins[1])
         next_logits(5, lin_bank[1])
         maximum(0, 6)
-        maximum(0, 7)
         gated(0, 2, lins[2])
         next_logits(2, lin_bank[2])
         next_logits(0, lin_bank[0])
+        next_logits(1, lin_bank[1])
+        maximum(0, 7)
         gated(0, 3, lins[3])
         next_logits(3, lin_bank[3])
-        next_logits(1, lin_bank[1])
         gated(0, 4, lins[4])
         next_logits(6, lin_bank[4])
         gated(0, 5, lins[5])
@@ -397,8 +397,7 @@ def tile_list_claim_count_rates_kernel(
         gated(1, 7, lins[7])
         finish(4)
         expose(*pieces[0][:2], done[0], nc.gpsimd, 1, 2, nc.sync)
-        expose(*pieces[1][:2], done[1], nc.gpsimd, 1, 2, nc.sync, 0, 2)
-        expose(*pieces[1][:2], done[1], nc.vector, 2, 2, nc.sync, 2, 4)
+        expose(*pieces[1][:2], done[1], nc.vector, 2, 2, nc.sync)
         expose(*pieces[2][:2], done[2], nc.vector, 2, 2, nc.scalar)
         expose(*pieces[3][:2], done[3], nc.vector, 4, 4, nc.scalar)
         expose(*pieces[4][:2], done[4], nc.vector, 2, 2, nc.scalar)

@@ -154,7 +154,7 @@ def tile_list_claim_count_rates_kernel(
         permute(w4_scale[:], w4_rows[:].bitcast(U8), 16)
         for q in range(4):
             nc.sync.dma_start(w4_low[32 * q : 32 * q + 4, :], w4_scale[32 * q + 4 : 32 * q + 8, :].bitcast(I32))
-        tab2 = [held([P, T2], I32, "reused%d" % c) for c in range(PASSES)]
+        tab2 = [held([P, T2], I32, name) for name in ("tab2_0", "reused1")]
         for c in range(PASSES):
             nc.sync.dma_start(tab2[c][:], tab2_words[c].rearrange("p t i -> p (t i)").bitcast(I32))
         bias = held([P, S2 // P], F32, "bias")
@@ -301,8 +301,7 @@ def tile_list_claim_count_rates_kernel(
         round_w1(raw11, 1, 1, nc.vector.tensor_copy)
         quantize_w1(0, 1)
         quantize_w1(1, 1)
-        gather_v2(0)
-        soft = held([P, BANKS, QUARTER, 2], F32, "reused0")
+        soft = held([P, BANKS, QUARTER, 2], F32, "w1_bf16_11")
 
         def logits(b, unit, k):
             z = bank(k, [P, 2, QUARTER])
@@ -354,6 +353,7 @@ def tile_list_claim_count_rates_kernel(
         gated(0, 7, lins[7])
         for half in range(2):
             quantize_h(0, half * HALF, HALF)
+        gather_v2(0)
         gather_v2(1)
         soft = held([P, BANKS, QUARTER, 2], F32, "reused1")
 

@@ -26,10 +26,9 @@ BLOCK = 128
 HALF = 512
 SLIVER = 64
 FLOOR_LOGIT = -41.0
-SCALAR_SHARE = 40
 AGAIN = ((6, 7), (4, 5))
 REPEAT_AFTER = (0, 2)
-SIGMOID_ORDER = ((0, 1, 2, 3, 4, 5, 6, 7), (4, 5, 2, 0, 1, 3, 6, 7))
+SIGMOID_ORDER = ((0, 1, 2, 3, 4, 5, 6, 7), (4, 5, 0, 1, 2, 3, 6, 7))
 
 
 def tile_list_claim_count_rates_kernel(
@@ -39,6 +38,7 @@ def tile_list_claim_count_rates_kernel(
     with ExitStack() as ctx:
         keep = ctx.enter_context(tc.tile_pool(name="keep", bufs=1))
         psum = ctx.enter_context(tc.psum_pool(name="psum", bufs=1))
+        shared = ctx.enter_context(tc.tile_pool(name="shared", bufs=1))
 
         def held(shape, dtype, name):
             return keep.tile(shape, dtype, name=name, align_bytes=256)
@@ -55,9 +55,9 @@ def tile_list_claim_count_rates_kernel(
         nc.vector.memset(floor[:, 0:1], FLOOR_LOGIT)
         nc.scalar.activation(floor[:, 8:9], floor[:, 0:1], ACT.Sigmoid)
 
-        w4_rows = held([P, H // 4], I32, "w4_rows")
+        w4_rows = held([P, PASSES, H // 4], I32, "w4_rows")
         tab2_rows = held([P, T2 // 4], I32, "tab2_rows")
-        w4_low = held([P, H // 4], I32, "w4_low")
+        w4_placed = held([P, PASSES, H // 4], I32, "w4_placed")
         v_scale = held([P, PASSES, S // 4], I32, "v_scale")
         v2_scale = held([P, S2 // 4], I32, "v2_scale")
 
@@ -75,11 +75,11 @@ def tile_list_claim_count_rates_kernel(
         def load_tab(a):
             nc.sync.dma_start(tab[a][:], tab_words[a].rearrange("p t i -> p (t i)").bitcast(I32))
 
-        def load_rows(rows, scales):
-            for q in range(4):
-                nc.sync.dma_start(rows[32 * q : 32 * q + 8, :], scales.bitcast(I32)[:, 4 * q : 4 * q + 4, :])
+        def placed(shape, dtype, name, quarter):
+            return shared.tile(shape, dtype, name=name, align_bytes=256, offset=quarter * 4096)
 
-        w1_bf16 = [[held([P, PACK, P, PACK], BF16, "w1_bf16_%d%d" % (a, b)) for b in range(PASSES)] for a in range(PASSES)]
+        w1_bf16 = [[held([P, PACK, P, PACK], BF16, "w1_bf16_0%d" % b) for b in range(PASSES)]]
+        w1_bf16.append([held([P, PACK, P, PACK], BF16, "w1_bf16_10"), placed([P, 4 * PACK, P, PACK], BF16, "w1_bf16_11", 0)[:, 0:PACK]])
 
         def round_w1(raw, a, b, copy, low=0, high=P):
             copy(
@@ -111,49 +111,48 @@ def tile_list_claim_count_rates_kernel(
         picked_rows = held([P, S], U8, "picked_rows")
         picked2_rows = held([P, S2], U8, "picked2_rows")
 
-        raw00 = load_w1(0, 0)
-        nc.sync.dma_start(holders[:], offs)
-        spread_rows(tab_rows, tab_scales)
-        nc.sync.dma_start(perils[:], offs2)
-        nc.vector.memset(tab2_rows[:], 0)
-        spread_rows(tab2_rows, tab2_scales)
-        load_tab(0)
-        load_tab(1)
-        nc.vector.memset(v_scale[:], 0)
-        nc.vector.tensor_copy(picked_rows[:], tab_rows[:].bitcast(U8).indirect(holders[:]))
-        place_rows(v_scale[:, 0, :], 0, picked_rows, 0)
-        raw10 = load_w1(1, 0)
-        place_rows(v_scale[:, 1, :], 0, picked_rows, 1)
-        nc.vector.tensor_copy(picked2_rows[:], tab2_rows[:].bitcast(U8).indirect(perils[:]))
-        round_w1(raw00, 0, 0, nc.scalar.copy)
-        quantize_w1(0, 0)
-        gather_v(0, 0)
-        gather_v(0, 1)
-        gather_v(1, 0)
-        gather_v(1, 1)
-        round_w1(raw10, 1, 0, nc.scalar.copy, 0, SCALAR_SHARE)
-        round_w1(raw10, 1, 0, nc.vector.tensor_copy, SCALAR_SHARE, P)
-        quantize_w1(1, 0, 0, 2)
-        quantize_w1(1, 0, 2, 4)
-
-        w4_raw = held([P, PASSES, H // 2], I32, "w4_raw")
-        nc.sync.dma_start(w4_raw[:], w4_words.bitcast(I32).rearrange("a p c -> p a c"))
-        nc.vector.memset(w4_rows[:], 0)
-        load_rows(w4_rows, w4_scales)
-        raw01 = load_w1(0, 1)
-        nc.vector.memset(w4_low[:], 0)
-
         def permute(dst, src, run):
             nc.vector.tensor_copy(
                 dst.rearrange("p (g t m i) -> p g m t i", t=PACK, m=P // run, i=run),
                 src.rearrange("p (g m i t) -> p g m t i", t=PACK, m=P // run, i=run),
             )
 
+        raw00 = load_w1(0, 0)
+        nc.sync.dma_start(holders[:], offs)
+        spread_rows(tab_rows, tab_scales)
+        nc.sync.dma_start(perils[:], offs2)
+        nc.vector.memset(tab2_rows[:], 0)
+        spread_rows(tab2_rows, tab2_scales)
+        nc.vector.memset(w4_rows[:], 0)
+        nc.sync.dma_start(w4_rows[0:P:8], w4_scales.bitcast(I32).rearrange("a q c -> q a c"))
+        raw10 = load_w1(1, 0)
+        load_tab(0)
+        nc.vector.memset(v_scale[:], 0)
+        nc.vector.tensor_copy(picked_rows[:], tab_rows[:].bitcast(U8).indirect(holders[:]))
+        place_rows(v_scale[:, 0, :], 0, picked_rows, 0)
+        load_tab(1)
+        place_rows(v_scale[:, 1, :], 0, picked_rows, 1)
+        nc.vector.tensor_copy(picked2_rows[:], tab2_rows[:].bitcast(U8).indirect(perils[:]))
+        w4_scale = held([P, PASSES * H], U8, "w4_scale")
+        permute(w4_scale[:], w4_rows[:].rearrange("p a c -> p (a c)").bitcast(U8), 16)
+        round_w1(raw00, 0, 0, nc.scalar.copy)
+        round_w1(raw10, 1, 0, nc.scalar.copy)
+        quantize_w1(0, 0)
+        gather_v(0, 0)
+        gather_v(0, 1)
+        quantize_w1(1, 0)
+        gather_v(1, 0)
+        gather_v(1, 1)
+
+        w4_raw = held([P, PASSES, H // 2], I32, "w4_raw")
+        nc.sync.dma_start(w4_raw[:], w4_words.bitcast(I32).rearrange("a p c -> p a c"))
+        raw01 = load_w1(0, 1)
         raw11 = load_w1(1, 1)
-        w4_scale = held([P, H], U8, "w4_scale")
-        permute(w4_scale[:], w4_rows[:].bitcast(U8), 16)
+        nc.vector.memset(w4_placed[:], 0)
         for q in range(4):
-            nc.sync.dma_start(w4_low[32 * q : 32 * q + 4, :], w4_scale[32 * q + 4 : 32 * q + 8, :].bitcast(I32))
+            nc.sync.dma_start(
+                w4_placed[32 * q : 32 * q + 4].rearrange("p a c -> p (a c)"), w4_scale[32 * q : 32 * q + 32 : 8, :].bitcast(I32)
+            )
         tab2 = [held([P, T2], I32, name) for name in ("tab2_0", "reused1")]
         for c in range(PASSES):
             nc.sync.dma_start(tab2[c][:], tab2_words[c].rearrange("p t i -> p (t i)").bitcast(I32))
@@ -170,7 +169,6 @@ def tile_list_claim_count_rates_kernel(
 
         h_codes = held([P, PASSES, S], U32, "h_codes")
         h_scale = held([P, PASSES, S], U8, "h_scale")
-        v2_words = held([P, PASSES, S2], U32, "v2_words")
         gate = held([P, BANKS, HALF + SLIVER], F32, "gate")
         h = [held([P, S, PACK], BF16, "h%d" % b) for b in range(PASSES)]
 
@@ -210,10 +208,10 @@ def tile_list_claim_count_rates_kernel(
 
         def softplus(b, k, z):
             nc.vector.scalar_tensor_tensor(
-                soft[:, k].rearrange("p (g n) e -> p g n e", g=BANKS), gate_of(b, k), -1.0, paired(z), ALU.mult, ALU.max
+                soft[k // 2][:, k % 2].rearrange("p (g n) e -> p g n e", g=BANKS), gate_of(b, k), -1.0, paired(z), ALU.mult, ALU.max
             )
 
-        w4_planes = [w4_scale[:], w4_low[:].bitcast(U8)]
+        w4_planes = [w4_placed[:, a, :].bitcast(U8) for a in range(PASSES)]
 
         def linear(b, j, k):
             lin = bank(k, [P, PACK, BLOCK])
@@ -236,7 +234,7 @@ def tile_list_claim_count_rates_kernel(
             nc.vector.tensor_tensor(
                 h[b][:, j * BLOCK : (j + 1) * BLOCK, :].rearrange("p n (u e) -> p n u e", e=2),
                 lin[:].rearrange("p (u e) n -> p n u e", e=2),
-                soft[:, 2 * quarter : 2 * quarter + 2, half * BLOCK : (half + 1) * BLOCK, :].rearrange("p u n e -> p n u e"),
+                soft[quarter][:, :, half * BLOCK : (half + 1) * BLOCK, :].rearrange("p u n e -> p n u e"),
                 ALU.mult,
             )
 
@@ -301,7 +299,7 @@ def tile_list_claim_count_rates_kernel(
         round_w1(raw11, 1, 1, nc.vector.tensor_copy)
         quantize_w1(0, 1)
         quantize_w1(1, 1)
-        soft = held([P, BANKS, QUARTER, 2], F32, "w1_bf16_11")
+        soft = [placed([P, 2, QUARTER, 2], F32, "soft%d" % quarter, quarter) for quarter in range(4)]
 
         def logits(b, unit, k):
             z = bank(k, [P, 2, QUARTER])
@@ -330,74 +328,80 @@ def tile_list_claim_count_rates_kernel(
             following[k] = (logits(1, k, place), place)
             sigmoid(1, k, following[k][0])
 
-        for n in range(5):
+        for n in range(4):
             maximum(0, n)
         gated(0, 0, lins[0])
-        next_logits(4, lin_bank[0])
-        maximum(0, 5)
+        next_logits(4, 6)
+        maximum(0, 4)
         gated(0, 1, lins[1])
-        next_logits(5, lin_bank[1])
-        maximum(0, 6)
+        next_logits(5, 7)
+        maximum(0, 5)
+        softplus(0, 6, zs[6])
+        next_logits(0, 0)
         gated(0, 2, lins[2])
-        next_logits(2, lin_bank[2])
-        next_logits(0, lin_bank[0])
-        next_logits(1, lin_bank[1])
-        maximum(0, 7)
+        next_logits(1, 2)
+        softplus(0, 7, zs[7])
+        next_logits(2, 1)
+        next_logits(3, 6)
         gated(0, 3, lins[3])
-        next_logits(3, lin_bank[3])
+        next_logits(6, 3)
+        next_logits(7, 7)
         gated(0, 4, lins[4])
-        next_logits(6, lin_bank[4])
+        lins.append(linear(0, 6, 4))
         gated(0, 5, lins[5])
-        next_logits(7, lin_bank[5])
-        gated(0, 6, lins[6])
-        gated(0, 7, lins[7])
-        for half in range(2):
-            quantize_h(0, half * HALF, HALF)
+        lins.append(linear(0, 7, 5))
+        v2_words = placed([P, PASSES, S2], U32, "v2_words", 2)
         gather_v2(0)
         gather_v2(1)
-        soft = held([P, BANKS, QUARTER, 2], F32, "reused1")
+        quantize_h(0, 0, HALF)
+        gated(0, 6, lins[6])
+        gated(0, 7, lins[7])
+        quantize_h(0, HALF, HALF)
+        whole = held([P, 4, 2, QUARTER, 2], F32, "reused1")
+        soft = [whole[:, quarter] for quarter in range(4)]
 
-        zs = [following[k][0] for k in range(BANKS)]
-        z_bank = [following[k][1] for k in range(BANKS)]
-        lin_bank = lin_bank[6:]
-        lins = [linear(1, j, k) for j, k in enumerate(lin_bank)]
+        zs = {k: following[k][0] for k in range(BANKS)}
+        lins = [linear(1, 0, 4), linear(1, 1, 5)]
         logs(1)
-        pieces = [
-            (0, QUARTER, (0, 1)),
-            (QUARTER, QUARTER, (2, 3)),
-            (2 * QUARTER, QUARTER, (4, 5)),
-            (6 * BLOCK, BLOCK, (0, 1)),
-            (7 * BLOCK, BLOCK, (2, 3, 6, 7)),
-        ]
+        pieces = [(0, QUARTER), (QUARTER, QUARTER), (2 * QUARTER, QUARTER), (6 * BLOCK, BLOCK), (7 * BLOCK, BLOCK)]
         done = []
 
-        def finish(piece):
-            first, width, freed = pieces[piece]
-            quantize_h(1, first, width)
-            done.append(rates(first, width, [lin_bank[j] for j in freed]))
-
-        for k in range(3):
-            maximum(1, k)
+        softplus(1, 0, zs[0])
+        lins.append(linear(1, 2, 0))
+        softplus(1, 1, zs[1])
+        lins.append(linear(1, 3, 2))
         gated(1, 0, lins[0])
+        zs[4] = logits(1, 4, 4)
         gated(1, 1, lins[1])
-        maximum(1, 3)
-        finish(0)
+        zs[5] = logits(1, 5, 5)
+        softplus(1, 2, zs[2])
+        quantize_h(1, *pieces[0])
+        softplus(1, 3, zs[3])
+        done.append(rates(*pieces[0], [1, 6]))
         gated(1, 2, lins[2])
+        lins.append(linear(1, 4, 0))
         gated(1, 3, lins[3])
-        maximum(1, 4)
-        finish(1)
-        maximum(1, 5)
-        maximum(1, 6)
-        maximum(1, 7)
+        lins.append(linear(1, 5, 2))
+        softplus(1, 4, zs[4])
+        quantize_h(1, *pieces[1])
+        softplus(1, 5, zs[5])
+        done.append(rates(*pieces[1], [4, 5]))
+        lins.append(linear(1, 6, 1))
+        lins.append(linear(1, 7, 6))
         gated(1, 4, lins[4])
         gated(1, 5, lins[5])
+        softplus(1, 6, zs[6])
+        quantize_h(1, *pieces[2])
+        done.append(rates(*pieces[2], [0, 2]))
+        softplus(1, 7, zs[7])
         gated(1, 6, lins[6])
-        finish(2)
-        finish(3)
+        quantize_h(1, *pieces[3])
+        done.append(rates(*pieces[3], [3, 7]))
         gated(1, 7, lins[7])
-        finish(4)
-        expose(*pieces[0][:2], done[0], nc.gpsimd, 1, 2, nc.sync)
-        expose(*pieces[1][:2], done[1], nc.vector, 2, 2, nc.sync)
-        expose(*pieces[2][:2], done[2], nc.vector, 2, 2, nc.scalar)
-        expose(*pieces[3][:2], done[3], nc.vector, 4, 4, nc.scalar)
-        expose(*pieces[4][:2], done[4], nc.vector, 2, 2, nc.scalar)
+        quantize_h(1, *pieces[4])
+        done.append(rates(*pieces[4], [4, 5, 1, 6]))
+        expose(*pieces[0], done[0], nc.gpsimd, 1, 2, nc.sync)
+        expose(*pieces[1], done[1], nc.vector, 2, 2, nc.sync)
+        expose(*pieces[2], done[2], nc.vector, 2, 2, nc.scalar)
+        expose(*pieces[3], done[3], nc.vector, 4, 4, nc.scalar)
+        expose(*pieces[4], done[4], nc.vector, 2, 2, nc.scalar)

@@ -335,73 +335,76 @@ def tile_list_claim_count_rates_kernel(
         maximum(0, 4)
         gated(0, 1, lins[1])
         next_logits(5, 7)
-        maximum(0, 5)
+        softplus(0, 5, zs[5])
+        next_logits(0, 5)
         softplus(0, 6, zs[6])
-        next_logits(0, 0)
+        next_logits(1, 0)
         gated(0, 2, lins[2])
-        next_logits(1, 2)
+        next_logits(2, 2)
         softplus(0, 7, zs[7])
-        next_logits(2, 1)
-        next_logits(3, 6)
-        gated(0, 3, lins[3])
-        next_logits(6, 3)
+        next_logits(3, 1)
+        next_logits(6, 6)
         next_logits(7, 7)
+        gated(0, 3, lins[3])
+        lins.append(linear(0, 5, 3))
         gated(0, 4, lins[4])
         lins.append(linear(0, 6, 4))
-        gated(0, 5, lins[5])
-        lins.append(linear(0, 7, 5))
-        v2_words = placed([P, PASSES, S2], U32, "v2_words", 2)
+        v2_words = placed([P, PASSES, S2], U32, "v2_words", 1)
         gather_v2(0)
         gather_v2(1)
+        gated(0, 5, lins[5])
+        lins.append(linear(0, 7, 3))
         quantize_h(0, 0, HALF)
         gated(0, 6, lins[6])
+        quantize_h(0, HALF, QUARTER)
         gated(0, 7, lins[7])
-        quantize_h(0, HALF, HALF)
+        quantize_h(0, HALF + QUARTER, QUARTER)
         whole = held([P, 4, 2, QUARTER, 2], F32, "reused1")
         soft = [whole[:, quarter] for quarter in range(4)]
 
         zs = {k: following[k][0] for k in range(BANKS)}
-        lins = [linear(1, 0, 4), linear(1, 1, 5)]
+        lins = [linear(1, 0, 4), linear(1, 1, 3)]
         logs(1)
         pieces = [(0, QUARTER), (QUARTER, QUARTER), (2 * QUARTER, QUARTER), (6 * BLOCK, BLOCK), (7 * BLOCK, BLOCK)]
         done = []
 
         softplus(1, 0, zs[0])
-        lins.append(linear(1, 2, 0))
+        lins.append(linear(1, 2, 5))
         softplus(1, 1, zs[1])
-        lins.append(linear(1, 3, 2))
+        lins.append(linear(1, 3, 0))
         gated(1, 0, lins[0])
         zs[4] = logits(1, 4, 4)
         gated(1, 1, lins[1])
-        zs[5] = logits(1, 5, 5)
+        zs[5] = logits(1, 5, 3)
         softplus(1, 2, zs[2])
         quantize_h(1, *pieces[0])
         softplus(1, 3, zs[3])
-        done.append(rates(*pieces[0], [1, 6]))
+        done.append(rates(*pieces[0], [2, 1]))
         gated(1, 2, lins[2])
-        lins.append(linear(1, 4, 0))
+        lins.append(linear(1, 4, 5))
         gated(1, 3, lins[3])
-        lins.append(linear(1, 5, 2))
+        lins.append(linear(1, 5, 0))
         softplus(1, 4, zs[4])
         quantize_h(1, *pieces[1])
         softplus(1, 5, zs[5])
-        done.append(rates(*pieces[1], [4, 5]))
-        lins.append(linear(1, 6, 1))
-        lins.append(linear(1, 7, 6))
+        done.append(rates(*pieces[1], [4, 3]))
+        lins.append(linear(1, 6, 2))
+        lins.append(linear(1, 7, 1))
         gated(1, 4, lins[4])
         gated(1, 5, lins[5])
         softplus(1, 6, zs[6])
         quantize_h(1, *pieces[2])
-        done.append(rates(*pieces[2], [0, 2]))
+        done.append(rates(*pieces[2], [5, 0]))
         softplus(1, 7, zs[7])
+        expose(*pieces[0], done[0], nc.gpsimd, 1, 2, nc.sync)
+        expose(*pieces[1], done[1], nc.gpsimd, 1, 2, nc.sync, 0, 2)
         gated(1, 6, lins[6])
+        expose(*pieces[1], done[1], nc.vector, 2, 2, nc.sync, 2, 4)
         quantize_h(1, *pieces[3])
-        done.append(rates(*pieces[3], [3, 7]))
+        done.append(rates(*pieces[3], [6, 7]))
         gated(1, 7, lins[7])
         quantize_h(1, *pieces[4])
-        done.append(rates(*pieces[4], [4, 5, 1, 6]))
-        expose(*pieces[0], done[0], nc.gpsimd, 1, 2, nc.sync)
-        expose(*pieces[1], done[1], nc.vector, 2, 2, nc.sync)
+        done.append(rates(*pieces[4], [4, 3, 2, 1]))
         expose(*pieces[2], done[2], nc.vector, 2, 2, nc.scalar)
         expose(*pieces[3], done[3], nc.vector, 4, 4, nc.scalar)
         expose(*pieces[4], done[4], nc.vector, 2, 2, nc.scalar)

@@ -147,15 +147,19 @@ def tile_list_claim_count_rates_kernel(
         w4_raw = held([P, PASSES, H // 2], I32, "w4_raw")
         nc.sync.dma_start(w4_raw[:], w4_words.bitcast(I32).rearrange("a p c -> p a c"))
         raw01 = load_w1(0, 1)
+        tab2 = [held([P, T2], I32, name) for name in ("tab2_0", "reused1")]
+
+        def load_tab2(c):
+            nc.sync.dma_start(tab2[c][:], tab2_words[c].rearrange("p t i -> p (t i)").bitcast(I32))
+
+        load_tab2(0)
         raw11 = load_w1(1, 1)
         nc.vector.memset(w4_placed[:], 0)
         for q in range(4):
             nc.sync.dma_start(
                 w4_placed[32 * q : 32 * q + 4].rearrange("p a c -> p (a c)"), w4_scale[32 * q : 32 * q + 32 : 8, :].bitcast(I32)
             )
-        tab2 = [held([P, T2], I32, name) for name in ("tab2_0", "reused1")]
-        for c in range(PASSES):
-            nc.sync.dma_start(tab2[c][:], tab2_words[c].rearrange("p t i -> p (t i)").bitcast(I32))
+        load_tab2(1)
         bias = held([P, S2 // P], F32, "bias")
         with nc.allow_non_contiguous_dma(reason="one bias value for each partition"):
             nc.sync.dma_start(bias[:], pb.rearrange("(i p) -> p i", p=P))
@@ -256,7 +260,7 @@ def tile_list_claim_count_rates_kernel(
                     for b in range(PASSES):
                         nc.tensor.matmul_mx(
                             out=y[:, e, :],
-                            lhsT=v2_words[:, b, i * P : (i + 1) * P].bitcast(FP8X4),
+                            lhsT=v2_words[b][:, i * P : (i + 1) * P].bitcast(FP8X4),
                             lhsT_scale=v2_scale[:].bitcast(U8)[4 * b :, i * P : (i + 1) * P],
                             rhs=h_codes[:, b, cols].bitcast(FP8X4),
                             rhs_scale=h_scale[:, b, cols],
@@ -293,11 +297,13 @@ def tile_list_claim_count_rates_kernel(
         )
 
         def gather_v2(c):
-            nc.vector.tensor_copy(v2_words[:, c, :], tab2[c][:].bitcast(U32).indirect(perils[:]))
+            nc.vector.tensor_copy(v2_words[c][:], tab2[c][:].bitcast(U32).indirect(perils[:]))
 
         round_w1(raw01, 0, 1, nc.vector.tensor_copy)
-        round_w1(raw11, 1, 1, nc.vector.tensor_copy)
         quantize_w1(0, 1)
+        v2_words = [held([P, S2], U32, "v2_words0")]
+        gather_v2(0)
+        round_w1(raw11, 1, 1, nc.vector.tensor_copy)
         quantize_w1(1, 1)
         soft = [placed([P, 2, QUARTER, 2], F32, "soft%d" % quarter, quarter) for quarter in range(4)]
 
@@ -349,8 +355,7 @@ def tile_list_claim_count_rates_kernel(
         lins.append(linear(0, 5, 3))
         gated(0, 4, lins[4])
         lins.append(linear(0, 6, 4))
-        v2_words = placed([P, PASSES, S2], U32, "v2_words", 1)
-        gather_v2(0)
+        v2_words.append(placed([P, S2], U32, "v2_words1", 1))
         gather_v2(1)
         gated(0, 5, lins[5])
         lins.append(linear(0, 7, 3))
@@ -397,7 +402,7 @@ def tile_list_claim_count_rates_kernel(
         done.append(rates(*pieces[2], [5, 0]))
         softplus(1, 7, zs[7])
         expose(*pieces[0], done[0], nc.gpsimd, 1, 2, nc.sync)
-        expose(*pieces[1], done[1], nc.gpsimd, 1, 2, nc.sync, 0, 2)
+        expose(*pieces[1], done[1], nc.vector, 2, 2, nc.sync, 0, 2)
         gated(1, 6, lins[6])
         expose(*pieces[1], done[1], nc.vector, 2, 2, nc.sync, 2, 4)
         quantize_h(1, *pieces[3])
@@ -405,6 +410,6 @@ def tile_list_claim_count_rates_kernel(
         gated(1, 7, lins[7])
         quantize_h(1, *pieces[4])
         done.append(rates(*pieces[4], [4, 3, 2, 1]))
-        expose(*pieces[2], done[2], nc.vector, 2, 2, nc.scalar)
-        expose(*pieces[3], done[3], nc.vector, 4, 4, nc.scalar)
-        expose(*pieces[4], done[4], nc.vector, 2, 2, nc.scalar)
+        expose(*pieces[2], done[2], nc.vector, 2, 2, nc.sync)
+        expose(*pieces[3], done[3], nc.vector, 4, 4, nc.sync)
+        expose(*pieces[4], done[4], nc.vector, 2, 2, nc.sync)

@@ -25,10 +25,11 @@ QUARTER = 256
 BLOCK = 128
 HALF = 512
 SLIVER = 64
+ROW = HALF + SLIVER
+GATE_ROW = ((0, 1, 2, 3, 4, 5, 6), (0, 1, 4, 5, 2, 3, 6))
 FLOOR_LOGIT = -41.0
 AGAIN = ((6, 7), (4, 5))
 REPEAT_AFTER = (0, 2)
-SIGMOID_ORDER = ((0, 1, 2, 3, 4, 5, 6, 7), (4, 5, 0, 1, 2, 3, 6, 7))
 
 
 def tile_list_claim_count_rates_kernel(
@@ -79,7 +80,7 @@ def tile_list_claim_count_rates_kernel(
             return shared.tile(shape, dtype, name=name, align_bytes=256, offset=quarter * 4096)
 
         w1_bf16 = [[held([P, PACK, P, PACK], BF16, "w1_bf16_0%d" % b) for b in range(PASSES)]]
-        w1_bf16.append([held([P, PACK, P, PACK], BF16, "w1_bf16_10"), placed([P, 4 * PACK, P, PACK], BF16, "w1_bf16_11", 0)[:, 0:PACK]])
+        w1_bf16.append([held([P, PACK, P, PACK], BF16, "w1_bf16_10"), held([P, PACK, P, PACK], BF16, "w1_bf16_11")])
 
         def round_w1(raw, a, b, copy, low=0, high=P):
             copy(
@@ -144,21 +145,21 @@ def tile_list_claim_count_rates_kernel(
         gather_v(1, 0)
         gather_v(1, 1)
 
+        raw01 = load_w1(0, 1)
+        raw11 = load_w1(1, 1)
         w4_raw = held([P, PASSES, H // 2], I32, "w4_raw")
         nc.sync.dma_start(w4_raw[:], w4_words.bitcast(I32).rearrange("a p c -> p a c"))
-        raw01 = load_w1(0, 1)
-        tab2 = [held([P, T2], I32, name) for name in ("tab2_0", "reused1")]
-
-        def load_tab2(c):
-            nc.sync.dma_start(tab2[c][:], tab2_words[c].rearrange("p t i -> p (t i)").bitcast(I32))
-
-        load_tab2(0)
-        raw11 = load_w1(1, 1)
         nc.vector.memset(w4_placed[:], 0)
         for q in range(4):
             nc.sync.dma_start(
                 w4_placed[32 * q : 32 * q + 4].rearrange("p a c -> p (a c)"), w4_scale[32 * q : 32 * q + 32 : 8, :].bitcast(I32)
             )
+        tab2 = [placed([P, 4, T2], I32, "tab2_0", 0)[:, 0], held([P, T2], I32, "reused1")[:]]
+
+        def load_tab2(c):
+            nc.sync.dma_start(tab2[c], tab2_words[c].rearrange("p t i -> p (t i)").bitcast(I32))
+
+        load_tab2(0)
         load_tab2(1)
         bias = held([P, S2 // P], F32, "bias")
         with nc.allow_non_contiguous_dma(reason="one bias value for each partition"):
@@ -179,9 +180,9 @@ def tile_list_claim_count_rates_kernel(
         v_planes = [v_scale[:, a, :].bitcast(U8) for a in range(PASSES)]
 
         def gate_of(b, k):
-            if k == SIGMOID_ORDER[b][-1]:
-                return gate[:, :, HALF:].rearrange("p g (n e) -> p g n e", e=2)
-            return gate[:, SIGMOID_ORDER[b].index(k), 0:HALF].rearrange("p (g n e) -> p g n e", g=BANKS, e=2)
+            if k == BANKS - 1:
+                return gate[:, :, 0:SLIVER].rearrange("p g (n e) -> p g n e", e=2)
+            return gate[:, GATE_ROW[b][k], SLIVER:].rearrange("p (g n e) -> p g n e", g=BANKS, e=2)
 
         def paired(z):
             return z[:].rearrange("p e (g n) -> p g n e", g=BANKS)
@@ -205,15 +206,16 @@ def tile_list_claim_count_rates_kernel(
             nc.scalar.activation(gate_of(b, k), paired(z), ACT.Sigmoid, scale=-1.0)
 
         def logs(b):
-            for k in range(BANKS):
-                row = SIGMOID_ORDER[b].index(k)
-                part = gate[:, row, HALF:] if row == BANKS - 1 else gate[:, row, :]
-                nc.scalar.activation(part, part, ACT.Ln, bias=floor[:, 8:9])
+            flat = gate[:].rearrange("p g c -> p (g c)")
+            spans = [(0, SLIVER + QUARTER), (SLIVER + QUARTER, ROW + SLIVER)]
+            spans = spans + [(row * ROW + SLIVER, (row + 1) * ROW + SLIVER) for row in GATE_ROW[b][1:]]
+            for low, high in spans:
+                nc.scalar.activation(flat[:, low:high], flat[:, low:high], ACT.Ln, bias=floor[:, 8:9])
 
         def softplus(b, k, z):
-            nc.vector.scalar_tensor_tensor(
-                soft[k // 2][:, k % 2].rearrange("p (g n) e -> p g n e", g=BANKS), gate_of(b, k), -1.0, paired(z), ALU.mult, ALU.max
-            )
+            target = soft[k // 2][:, k % 2].rearrange("p (g n) e -> p g n e", g=BANKS)
+            for part in [slice(0, BANKS // 2), slice(BANKS // 2, BANKS)] if k == 0 else [slice(0, BANKS)]:
+                nc.vector.scalar_tensor_tensor(target[:, part], gate_of(b, k)[:, part], -1.0, paired(z)[:, part], ALU.mult, ALU.max)
 
         w4_planes = [w4_placed[:, a, :].bitcast(U8) for a in range(PASSES)]
 
@@ -290,6 +292,9 @@ def tile_list_claim_count_rates_kernel(
         for k in range(BANKS):
             logit_pass(zs[k], 0, k, 1)
             sigmoid(0, k, zs[k])
+        round_w1(raw01, 0, 1, nc.vector.tensor_copy)
+        quantize_w1(0, 1)
+        round_w1(raw11, 1, 1, nc.vector.tensor_copy)
         permute(
             w4_codes[:].rearrange("p a b t c -> p (a b t c)").bitcast(U16),
             w4_raw[:].rearrange("p a c -> p (a c)").bitcast(U16),
@@ -297,13 +302,10 @@ def tile_list_claim_count_rates_kernel(
         )
 
         def gather_v2(c):
-            nc.vector.tensor_copy(v2_words[c][:], tab2[c][:].bitcast(U32).indirect(perils[:]))
+            nc.vector.tensor_copy(v2_words[c][:], tab2[c].bitcast(U32).indirect(perils[:]))
 
-        round_w1(raw01, 0, 1, nc.vector.tensor_copy)
-        quantize_w1(0, 1)
         v2_words = [held([P, S2], U32, "v2_words0")]
         gather_v2(0)
-        round_w1(raw11, 1, 1, nc.vector.tensor_copy)
         quantize_w1(1, 1)
         soft = [placed([P, 2, QUARTER, 2], F32, "soft%d" % quarter, quarter) for quarter in range(4)]
 
@@ -398,16 +400,16 @@ def tile_list_claim_count_rates_kernel(
         gated(1, 4, lins[4])
         gated(1, 5, lins[5])
         softplus(1, 6, zs[6])
+        softplus(1, 7, zs[7])
         quantize_h(1, *pieces[2])
         done.append(rates(*pieces[2], [5, 0]))
-        softplus(1, 7, zs[7])
+        gated(1, 6, lins[6])
         expose(*pieces[0], done[0], nc.gpsimd, 1, 2, nc.sync)
         expose(*pieces[1], done[1], nc.vector, 2, 2, nc.sync, 0, 2)
-        gated(1, 6, lins[6])
-        expose(*pieces[1], done[1], nc.vector, 2, 2, nc.sync, 2, 4)
         quantize_h(1, *pieces[3])
         done.append(rates(*pieces[3], [6, 7]))
         gated(1, 7, lins[7])
+        expose(*pieces[1], done[1], nc.vector, 2, 2, nc.sync, 2, 4)
         quantize_h(1, *pieces[4])
         done.append(rates(*pieces[4], [4, 3, 2, 1]))
         expose(*pieces[2], done[2], nc.vector, 2, 2, nc.sync)

@@ -84,8 +84,8 @@ def tile_list_claim_count_rates_kernel(
 
         def round_w1(raw, a, b, copy, low=0, high=P):
             copy(
-                w1_bf16[a][b][:, :, low:high, :].rearrange("p t m j -> p m t j"),
-                raw[:].rearrange("p j (m t) -> p m t j", t=PACK)[:, low:high],
+                w1_bf16[a][b][:, :, low:high, :].rearrange("p t m j -> p m j t"),
+                raw[:].rearrange("p j (m t) -> p m j t", t=PACK)[:, low:high],
             )
 
         def quantize_w1(a, b, low=0, high=PACK):

@@ -154,7 +154,7 @@ def tile_list_claim_count_rates_kernel(
             nc.sync.dma_start(
                 w4_placed[32 * q : 32 * q + 4].rearrange("p a c -> p (a c)"), w4_scale[32 * q : 32 * q + 32 : 8, :].bitcast(I32)
             )
-        tab2 = [placed([P, 4, T2], I32, "tab2_0", 0)[:, 0], held([P, T2], I32, "reused1")[:]]
+        tab2 = [placed([P, 5, T2], I32, "tab2_0", 0)[:, 0], held([P, T2], I32, "reused1")[:]]
 
         def load_tab2(c):
             nc.sync.dma_start(tab2[c], tab2_words[c].rearrange("p t i -> p (t i)").bitcast(I32))
@@ -170,12 +170,20 @@ def tile_list_claim_count_rates_kernel(
         for a in range(PASSES):
             place_rows(v2_scale, 4 * a, picked2_rows, a)
 
-        w4_codes = held([P, PASSES, PASSES, PACK, 2 * P], U8, "w4_codes")
+        w4_codes = []
 
         h_codes = held([P, PASSES, S], U32, "h_codes")
         h_scale = held([P, PASSES, S], U8, "h_scale")
         gate = held([P, BANKS, HALF + SLIVER], F32, "gate")
-        h = [held([P, S, PACK], BF16, "h%d" % b) for b in range(PASSES)]
+        h_first = held([P, S, PACK], BF16, "h0")
+        h_second = [held([P, QUARTER, PACK], BF16, "h1_%d" % quarter) for quarter in range(4)]
+
+        def h_of(b, first, width):
+            if b == 0:
+                return h_first[:, first : first + width, :]
+            quarter, low = divmod(first, QUARTER)
+            return h_second[quarter][:, low : low + width, :]
+
 
         v_planes = [v_scale[:, a, :].bitcast(U8) for a in range(PASSES)]
 
@@ -226,7 +234,7 @@ def tile_list_claim_count_rates_kernel(
                 for a in range(PASSES):
                     nc.tensor.matmul_mx(
                         out=lin[:, t, :],
-                        lhsT=w4_codes[:, a, b, t, :].bitcast(FP4X4),
+                        lhsT=w4_codes[b][:, a, t, :].bitcast(FP4X4),
                         lhsT_scale=w4_planes[a][:, b * PASS + t * P : b * PASS + (t + 1) * P],
                         rhs=v_words[a][:, picked].bitcast(FP8X4),
                         rhs_scale=v_planes[a][:, picked],
@@ -238,7 +246,7 @@ def tile_list_claim_count_rates_kernel(
         def gated(b, j, lin):
             quarter, half = divmod(j, 2)
             nc.vector.tensor_tensor(
-                h[b][:, j * BLOCK : (j + 1) * BLOCK, :].rearrange("p n (u e) -> p n u e", e=2),
+                h_of(b, j * BLOCK, BLOCK).rearrange("p n (u e) -> p n u e", e=2),
                 lin[:].rearrange("p (u e) n -> p n u e", e=2),
                 soft[quarter][:, :, half * BLOCK : (half + 1) * BLOCK, :].rearrange("p u n e -> p n u e"),
                 ALU.mult,
@@ -248,30 +256,29 @@ def tile_list_claim_count_rates_kernel(
             nc.vector.quantize_mx(
                 out=h_codes[:, b, first : first + width].bitcast(FP8X4),
                 scales=h_scale[:, b, first : first + width],
-                in_=h[b][:, first : first + width, :].rearrange("p n t -> p (n t)"),
+                in_=h_of(b, first, width).rearrange("p n t -> p (n t)"),
             )
 
         def rates(first, width, banks):
             cols = slice(first, first + width)
             tiles_in_bank = PACK // len(banks)
             counts = held([P, PACK, width], F32, "counts%d" % first)
-            for group, k in enumerate(banks):
-                y = bank(k, [P, tiles_in_bank, width])
-                for e in range(tiles_in_bank):
-                    i = tiles_in_bank * group + e
-                    for b in range(PASSES):
-                        nc.tensor.matmul_mx(
-                            out=y[:, e, :],
-                            lhsT=v2_words[b][:, i * P : (i + 1) * P].bitcast(FP8X4),
-                            lhsT_scale=v2_scale[:].bitcast(U8)[4 * b :, i * P : (i + 1) * P],
-                            rhs=h_codes[:, b, cols].bitcast(FP8X4),
-                            rhs_scale=h_scale[:, b, cols],
-                            start=(b == 0),
-                            stop=(b == PASSES - 1),
-                        )
-                for e in range(tiles_in_bank):
-                    i = tiles_in_bank * group + e
-                    nc.scalar.activation(counts[:, i, :], y[:, e, :], ACT.Exp, bias=bias[:, i : i + 1])
+            ys = [bank(k, [P, tiles_in_bank, width]) for k in banks]
+            for b in range(PASSES):
+                for i in range(PACK):
+                    group, e = divmod(i, tiles_in_bank)
+                    nc.tensor.matmul_mx(
+                        out=ys[group][:, e, :],
+                        lhsT=v2_words[b][:, i * P : (i + 1) * P].bitcast(FP8X4),
+                        lhsT_scale=v2_scale[:].bitcast(U8)[4 * b :, i * P : (i + 1) * P],
+                        rhs=h_codes[:, b, cols].bitcast(FP8X4),
+                        rhs_scale=h_scale[:, b, cols],
+                        start=(b == 0 and e == 0),
+                        stop=(b == PASSES - 1 and e == tiles_in_bank - 1),
+                    )
+            for i in range(PACK):
+                group, e = divmod(i, tiles_in_bank)
+                nc.scalar.activation(counts[:, i, :], ys[group][:, e, :], ACT.Exp, bias=bias[:, i : i + 1])
             return counts
 
         def expose(first, width, counts, engine, tiles, stored, queue, low_tile=0, high_tile=PACK):
@@ -295,10 +302,11 @@ def tile_list_claim_count_rates_kernel(
         round_w1(raw01, 0, 1, nc.vector.tensor_copy)
         quantize_w1(0, 1)
         round_w1(raw11, 1, 1, nc.vector.tensor_copy)
-        permute(
-            w4_codes[:].rearrange("p a b t c -> p (a b t c)").bitcast(U16),
-            w4_raw[:].rearrange("p a c -> p (a c)").bitcast(U16),
-            8,
+        quantize_w1(1, 1)
+        w4_codes.append(held([P, PASSES, PACK, 2 * P], U8, "w1_bf16_11"))
+        nc.vector.tensor_copy(
+            w4_codes[0][:].bitcast(U16).rearrange("p a t (m i) -> p a m t i", i=8),
+            w4_raw[:, :, 0 : H // 4].bitcast(U16).rearrange("p a (m i t) -> p a m t i", t=PACK, i=8),
         )
 
         def gather_v2(c):
@@ -306,7 +314,13 @@ def tile_list_claim_count_rates_kernel(
 
         v2_words = [held([P, S2], U32, "v2_words0")]
         gather_v2(0)
-        quantize_w1(1, 1)
+        w4_codes.append(placed([P, PASSES, PACK, 2 * P], U8, "w4_codes1", 4))
+        for a in range(PASSES):
+            for u in range(2):
+                nc.gpsimd.tensor_copy(
+                    w4_codes[1][:, a, 2 * u : 2 * u + 2, :].rearrange("p t (m y) -> p t m y", y=2),
+                    w4_raw[:, a, H // 4 :].bitcast(U8).rearrange("p (m t y) -> p t m y", t=PACK, y=2)[:, 2 * u : 2 * u + 2],
+                )
         soft = [placed([P, 2, QUARTER, 2], F32, "soft%d" % quarter, quarter) for quarter in range(4)]
 
         def logits(b, unit, k):
@@ -398,20 +412,24 @@ def tile_list_claim_count_rates_kernel(
         lins.append(linear(1, 6, 2))
         lins.append(linear(1, 7, 1))
         gated(1, 4, lins[4])
-        gated(1, 5, lins[5])
         softplus(1, 6, zs[6])
         softplus(1, 7, zs[7])
+        gated(1, 5, lins[5])
+        gated(1, 6, lins[6])
         quantize_h(1, *pieces[2])
         done.append(rates(*pieces[2], [5, 0]))
-        gated(1, 6, lins[6])
-        expose(*pieces[0], done[0], nc.gpsimd, 1, 2, nc.sync)
-        expose(*pieces[1], done[1], nc.vector, 2, 2, nc.sync, 0, 2)
+        shifted = [held([P, 2, QUARTER], F32, "h1_1")[:], done[0][:, 0:2, :]]
+        for n in range(2):
+            factor = exposure[:, 0:QUARTER].unsqueeze(1).to_broadcast([P, 2, QUARTER])
+            nc.gpsimd.tensor_tensor(shifted[n], done[0][:, 2 * n : 2 * n + 2, :], factor, ALU.mult)
+            nc.sync.dma_start(out[2 * n * P : (2 * n + 2) * P, 0:QUARTER].rearrange("(i p) n -> p i n", p=P), shifted[n])
         quantize_h(1, *pieces[3])
         done.append(rates(*pieces[3], [6, 7]))
         gated(1, 7, lins[7])
-        expose(*pieces[1], done[1], nc.vector, 2, 2, nc.sync, 2, 4)
+        expose(*pieces[1], done[1], nc.vector, 2, 2, nc.sync, 0, 2)
         quantize_h(1, *pieces[4])
         done.append(rates(*pieces[4], [4, 3, 2, 1]))
+        expose(*pieces[1], done[1], nc.vector, 2, 2, nc.sync, 2, 4)
         expose(*pieces[2], done[2], nc.vector, 2, 2, nc.sync)
         expose(*pieces[3], done[3], nc.vector, 4, 4, nc.sync)
         expose(*pieces[4], done[4], nc.vector, 2, 2, nc.sync)

@@ -215,14 +215,14 @@ def tile_list_claim_count_rates_kernel(
 
         def logs(b):
             flat = gate[:].rearrange("p g c -> p (g c)")
-            spans = [(0, SLIVER + QUARTER), (SLIVER + QUARTER, ROW + SLIVER)]
+            spans = [(0, SLIVER + BLOCK), (SLIVER + BLOCK, ROW + SLIVER)] if b == 1 else [(0, ROW + SLIVER)]
             spans = spans + [(row * ROW + SLIVER, (row + 1) * ROW + SLIVER) for row in GATE_ROW[b][1:]]
             for low, high in spans:
                 nc.scalar.activation(flat[:, low:high], flat[:, low:high], ACT.Ln, bias=floor[:, 8:9])
 
         def softplus(b, k, z):
             target = soft[k // 2][:, k % 2].rearrange("p (g n) e -> p g n e", g=BANKS)
-            for part in [slice(0, BANKS // 2), slice(BANKS // 2, BANKS)] if k == 0 else [slice(0, BANKS)]:
+            for part in [slice(0, 2), slice(2, BANKS)] if (b, k) == (1, 0) else [slice(0, BANKS)]:
                 nc.vector.scalar_tensor_tensor(target[:, part], gate_of(b, k)[:, part], -1.0, paired(z)[:, part], ALU.mult, ALU.max)
 
         w4_planes = [w4_placed[:, a, :].bitcast(U8) for a in range(PASSES)]
@@ -406,29 +406,29 @@ def tile_list_claim_count_rates_kernel(
         gated(1, 3, lins[3])
         lins.append(linear(1, 5, 0))
         softplus(1, 4, zs[4])
+        lins.append(linear(1, 6, 4))
         quantize_h(1, *pieces[1])
         softplus(1, 5, zs[5])
-        done.append(rates(*pieces[1], [4, 3]))
-        lins.append(linear(1, 6, 2))
-        lins.append(linear(1, 7, 1))
+        lins.append(linear(1, 7, 3))
         gated(1, 4, lins[4])
         softplus(1, 6, zs[6])
+        done.append(rates(*pieces[1], [5, 6]))
         softplus(1, 7, zs[7])
         gated(1, 5, lins[5])
         gated(1, 6, lins[6])
         quantize_h(1, *pieces[2])
-        done.append(rates(*pieces[2], [5, 0]))
+        done.append(rates(*pieces[2], [7, 0]))
         shifted = [held([P, 2, QUARTER], F32, "h1_1")[:], done[0][:, 0:2, :]]
         for n in range(2):
             factor = exposure[:, 0:QUARTER].unsqueeze(1).to_broadcast([P, 2, QUARTER])
             nc.gpsimd.tensor_tensor(shifted[n], done[0][:, 2 * n : 2 * n + 2, :], factor, ALU.mult)
             nc.sync.dma_start(out[2 * n * P : (2 * n + 2) * P, 0:QUARTER].rearrange("(i p) n -> p i n", p=P), shifted[n])
         quantize_h(1, *pieces[3])
-        done.append(rates(*pieces[3], [6, 7]))
+        done.append(rates(*pieces[3], [2, 1]))
         gated(1, 7, lins[7])
         expose(*pieces[1], done[1], nc.vector, 2, 2, nc.sync, 0, 2)
         quantize_h(1, *pieces[4])
-        done.append(rates(*pieces[4], [4, 3, 2, 1]))
+        done.append(rates(*pieces[4], [4, 5, 6, 3]))
         expose(*pieces[1], done[1], nc.vector, 2, 2, nc.sync, 2, 4)
         expose(*pieces[2], done[2], nc.vector, 2, 2, nc.sync)
         expose(*pieces[3], done[3], nc.vector, 4, 4, nc.sync)

@@ -259,10 +259,10 @@ def tile_list_claim_count_rates_kernel(
                 in_=h_of(b, first, width).rearrange("p n t -> p (n t)"),
             )
 
-        def rates(first, width, banks):
+        def rates(first, width, banks, counts=None):
             cols = slice(first, first + width)
             tiles_in_bank = PACK // len(banks)
-            counts = held([P, PACK, width], F32, "counts%d" % first)
+            counts = held([P, PACK, width], F32, "counts%d" % first) if counts is None else counts
             ys = [bank(k, [P, tiles_in_bank, width]) for k in banks]
             for b in range(PASSES):
                 for i in range(PACK):
@@ -424,12 +424,13 @@ def tile_list_claim_count_rates_kernel(
             nc.gpsimd.tensor_tensor(shifted[n], done[0][:, 2 * n : 2 * n + 2, :], factor, ALU.mult)
             nc.sync.dma_start(out[2 * n * P : (2 * n + 2) * P, 0:QUARTER].rearrange("(i p) n -> p i n", p=P), shifted[n])
         quantize_h(1, *pieces[3])
-        done.append(rates(*pieces[3], [2, 1]))
+        last = held([P, PACK, QUARTER], F32, "counts_last")
+        rates(*pieces[3], [2, 1], last[:, :, 0:BLOCK])
         gated(1, 7, lins[7])
         expose(*pieces[1], done[1], nc.vector, 2, 2, nc.sync, 0, 2)
         quantize_h(1, *pieces[4])
-        done.append(rates(*pieces[4], [4, 5, 6, 3]))
+        rates(*pieces[4], [4, 5, 6, 3], last[:, :, BLOCK:])
         expose(*pieces[1], done[1], nc.vector, 2, 2, nc.sync, 2, 4)
         expose(*pieces[2], done[2], nc.vector, 2, 2, nc.sync)
-        expose(*pieces[3], done[3], nc.vector, 4, 4, nc.sync)
-        expose(*pieces[4], done[4], nc.vector, 2, 2, nc.sync)
+        expose(3 * QUARTER, QUARTER, last, nc.vector, 2, 2, nc.sync, 0, 2)
+        expose(3 * QUARTER, QUARTER, last, nc.vector, 1, 1, nc.sync, 2, 4)

from contextlib import ExitStack

import concourse.mybir as mybir

F32 = mybir.dt.float32
BF16 = mybir.dt.bfloat16
I32 = mybir.dt.int32
U32 = mybir.dt.uint32
U16 = mybir.dt.uint16
U8 = mybir.dt.uint8
FP8X4 = mybir.dt.float8_e4m3fn_x4
FP4X4 = mybir.dt.float4_e2m1fn_x4
ACT = mybir.ActivationFunctionType
ALU = mybir.AluOpType

K, H, T, S, T2, S2 = 1024, 1024, 4096, 1024, 1024, 512
FLOPS = 2 * K * H * S * 2 + 2 * H * S2 * S

P = 128
PACK = 4
PASS = P * PACK
PASSES = 2
BANKS = 8
QUARTER = 256
BLOCK = 128
HALF = 512
SLIVER = 64
ROW = HALF + SLIVER
GATE_ROW = ((0, 1, 2, 3, 4, 5, 6), (0, 1, 4, 5, 2, 3, 6))
FLOOR_LOGIT = -41.0
AGAIN = ((6, 7), (4, 5))
REPEAT_AFTER = (0, 2)


def tile_list_claim_count_rates_kernel(
    tc, tab_words, tab_scales, offs, tab2_words, tab2_scales, offs2, w1, w4_words, w4_scales, pb, ex, out
):
    nc = tc.nc
    with ExitStack() as ctx:
        keep = ctx.enter_context(tc.tile_pool(name="keep", bufs=1))
        psum = ctx.enter_context(tc.psum_pool(name="psum", bufs=1))
        shared = ctx.enter_context(tc.tile_pool(name="shared", bufs=1))

        def held(shape, dtype, name):
            return keep.tile(shape, dtype, name=name, align_bytes=256)

        def bank(k, shape):
            return psum.tile(shape, F32, name="bank%d" % k)

        holders = keep.tile([P, S // 16], U16, name="holders")
        perils = keep.tile([P, S2 // 16], U16, name="perils")

        tab_rows = held([P, T // 4], I32, "tab_rows")
        nc.vector.memset(tab_rows[:], 0)
        floor = held([P, 16], F32, "floor")
        nc.vector.memset(floor[:, 0:1], FLOOR_LOGIT)
        nc.scalar.activation(floor[:, 8:9], floor[:, 0:1], ACT.Sigmoid)

        w4_rows = held([P, PASSES, H // 4], I32, "w4_rows")
        tab2_rows = held([P, T2 // 4], I32, "tab2_rows")
        w4_placed = held([P, PASSES, H // 4], I32, "w4_placed")
        v_scale = held([P, PASSES, S // 4], I32, "v_scale")
        v2_scale = held([P, S2 // 4], I32, "v2_scale")

        tab = [held([P, T], I32, "tab%d" % a) for a in range(PASSES)]
        v_words = [held([P, S], U32, "v_words%d" % a) for a in range(PASSES)]
        w1_codes = held([P, PASSES, PASSES, PASS], U32, "w1_codes")
        w1_scale = held([P, PASSES, PASSES, PASS], U8, "w1_scale")

        def load_w1(a, b):
            raw = held([P, PACK, PASS], F32, "w1_raw%d%d" % (a, b))
            rows = w1[a * PASS : (a + 1) * PASS, b * PASS : (b + 1) * PASS]
            nc.sync.dma_start(raw[:], rows.rearrange("(p j) c -> p j c", j=PACK))
            return raw

        def load_tab(a):
            nc.sync.dma_start(tab[a][:], tab_words[a].rearrange("p t i -> p (t i)").bitcast(I32))

        def placed(shape, dtype, name, quarter):
            return shared.tile(shape, dtype, name=name, align_bytes=256, offset=quarter * 4096)

        w1_bf16 = [[held([P, PACK, P, PACK], BF16, "w1_bf16_0%d" % b) for b in range(PASSES)]]
        w1_bf16.append([held([P, PACK, P, PACK], BF16, "w1_bf16_10"), held([P, PACK, P, PACK], BF16, "w1_bf16_11")])

        def round_w1(raw, a, b, copy, low=0, high=P):
            copy(
                w1_bf16[a][b][:, :, low:high, :].rearrange("p t m j -> p m j t"),
                raw[:].rearrange("p j (m t) -> p m j t", t=PACK)[:, low:high],
            )

        def quantize_w1(a, b, low=0, high=PACK):
            nc.vector.quantize_mx(
                out=w1_codes[:, b, a, low * P : high * P].bitcast(FP8X4),
                scales=w1_scale[:, b, a, low * P : high * P],
                in_=w1_bf16[a][b][:, low:high].rearrange("p t m j -> p (t m j)"),
            )

        def gather_v(a, half):
            nc.vector.tensor_copy(
                v_words[a][:, half * HALF : (half + 1) * HALF],
                tab[a][:].bitcast(U32).indirect(holders[:, half * HALF // 16 : (half + 1) * HALF // 16]),
            )

        def spread_rows(rows, scales):
            nc.sync.dma_start(rows[0:P:4, :], scales.rearrange("a q t -> (a q) t").bitcast(I32))

        def place_rows(dst, low, picked, a):
            for q in range(4):
                first = 64 * a + 16 * q
                nc.sync.dma_start(dst[32 * q + low : 32 * q + low + 4, :], picked[first : first + 16 : 4, :].bitcast(I32))

        picked_rows = held([P, S], U8, "picked_rows")
        picked2_rows = held([P, S2], U8, "picked2_rows")

        def permute(dst, src, run):
            nc.vector.tensor_copy(
                dst.rearrange("p (g t m i) -> p g m t i", t=PACK, m=P // run, i=run),
                src.rearrange("p (g m i t) -> p g m t i", t=PACK, m=P // run, i=run),
            )

        raw00 = load_w1(0, 0)
        nc.sync.dma_start(holders[:], offs)
        spread_rows(tab_rows, tab_scales)
        nc.sync.dma_start(perils[:], offs2)
        nc.vector.memset(tab2_rows[:], 0)
        spread_rows(tab2_rows, tab2_scales)
        nc.vector.memset(w4_rows[:], 0)
        nc.sync.dma_start(w4_rows[0:P:8], w4_scales.bitcast(I32).rearrange("a q c -> q a c"))
        raw10 = load_w1(1, 0)
        load_tab(0)
        nc.vector.memset(v_scale[:], 0)
        nc.vector.tensor_copy(picked_rows[:], tab_rows[:].bitcast(U8).indirect(holders[:]))
        place_rows(v_scale[:, 0, :], 0, picked_rows, 0)
        load_tab(1)
        place_rows(v_scale[:, 1, :], 0, picked_rows, 1)
        nc.vector.tensor_copy(picked2_rows[:], tab2_rows[:].bitcast(U8).indirect(perils[:]))
        w4_scale = held([P, PASSES * H], U8, "w4_scale")
        permute(w4_scale[:], w4_rows[:].rearrange("p a c -> p (a c)").bitcast(U8), 16)
        round_w1(raw00, 0, 0, nc.scalar.copy)
        round_w1(raw10, 1, 0, nc.scalar.copy)
        quantize_w1(0, 0)
        gather_v(0, 0)
        gather_v(0, 1)
        quantize_w1(1, 0)
        gather_v(1, 0)
        gather_v(1, 1)

        raw01 = load_w1(0, 1)
        raw11 = load_w1(1, 1)
        w4_raw = held([P, PASSES, H // 2], I32, "w4_raw")
        nc.sync.dma_start(w4_raw[:], w4_words.bitcast(I32).rearrange("a p c -> p a c"))
        nc.vector.memset(w4_placed[:], 0)
        for q in range(4):
            nc.sync.dma_start(
                w4_placed[32 * q : 32 * q + 4].rearrange("p a c -> p (a c)"), w4_scale[32 * q : 32 * q + 32 : 8, :].bitcast(I32)
            )
        tab2 = [placed([P, 5, T2], I32, "tab2_0", 0)[:, 0], held([P, T2], I32, "reused1")[:]]

        def load_tab2(c):
            nc.sync.dma_start(tab2[c], tab2_words[c].rearrange("p t i -> p (t i)").bitcast(I32))

        load_tab2(0)
        load_tab2(1)
        bias = held([P, S2 // P], F32, "bias")
        with nc.allow_non_contiguous_dma(reason="one bias value for each partition"):
            nc.sync.dma_start(bias[:], pb.rearrange("(i p) -> p i", p=P))
        exposure = held([P, S], F32, "exposure")
        nc.sync.dma_start(exposure[:], ex.partition_broadcast(P))
        nc.vector.memset(v2_scale[:], 0)
        for a in range(PASSES):
            place_rows(v2_scale, 4 * a, picked2_rows, a)

        w4_codes = []

        h_codes = held([P, PASSES, S], U32, "h_codes")
        h_scale = held([P, PASSES, S], U8, "h_scale")
        gate = held([P, BANKS, HALF + SLIVER], F32, "gate")
        h_first = held([P, S, PACK], BF16, "h0")
        h_second = [held([P, QUARTER, PACK], BF16, "h1_%d" % quarter) for quarter in range(4)]

        def h_of(b, first, width):
            if b == 0:
                return h_first[:, first : first + width, :]
            quarter, low = divmod(first, QUARTER)
            return h_second[quarter][:, low : low + width, :]


        v_planes = [v_scale[:, a, :].bitcast(U8) for a in range(PASSES)]

        def gate_of(b, k):
            if k == BANKS - 1:
                return gate[:, :, 0:SLIVER].rearrange("p g (n e) -> p g n e", e=2)
            return gate[:, GATE_ROW[b][k], SLIVER:].rearrange("p (g n e) -> p g n e", g=BANKS, e=2)

        def paired(z):
            return z[:].rearrange("p e (g n) -> p g n e", g=BANKS)

        def logit_pass(z, b, k, a):
            quarter, u = divmod(k, 2)
            picked = slice(quarter * QUARTER, (quarter + 1) * QUARTER)
            for e in range(2):
                cols = slice((2 * u + e) * P, (2 * u + e + 1) * P)
                nc.tensor.matmul_mx(
                    out=z[:, e, :],
                    lhsT=w1_codes[:, b, a, cols].bitcast(FP8X4),
                    lhsT_scale=w1_scale[:, b, a, cols],
                    rhs=v_words[a][:, picked].bitcast(FP8X4),
                    rhs_scale=v_planes[a][:, picked],
                    start=(a == 0 and e == 0),
                    stop=(a == PASSES - 1 and e == 1),
                )

        def sigmoid(b, k, z):
            nc.scalar.activation(gate_of(b, k), paired(z), ACT.Sigmoid, scale=-1.0)

        def logs(b):
            flat = gate[:].rearrange("p g c -> p (g c)")
            spans = [(0, SLIVER + BLOCK), (SLIVER + BLOCK, ROW + SLIVER)] if b == 1 else [(0, ROW + SLIVER)]
            spans = spans + [(row * ROW + SLIVER, (row + 1) * ROW + SLIVER) for row in GATE_ROW[b][1:]]
            for low, high in spans:
                nc.scalar.activation(flat[:, low:high], flat[:, low:high], ACT.Ln, bias=floor[:, 8:9])

        def softplus(b, k, z):
            target = soft[k // 2][:, k % 2].rearrange("p (g n) e -> p g n e", g=BANKS)
            for part in [slice(0, 2), slice(2, BANKS)] if (b, k) == (1, 0) else [slice(0, BANKS)]:
                nc.vector.scalar_tensor_tensor(target[:, part], gate_of(b, k)[:, part], -1.0, paired(z)[:, part], ALU.mult, ALU.max)

        w4_planes = [w4_placed[:, a, :].bitcast(U8) for a in range(PASSES)]

        def linear(b, j, k):
            lin = bank(k, [P, PACK, BLOCK])
            picked = slice(j * BLOCK, (j + 1) * BLOCK)
            for t in range(PACK):
                for a in range(PASSES):
                    nc.tensor.matmul_mx(
                        out=lin[:, t, :],
                        lhsT=w4_codes[b][:, a, t, :].bitcast(FP4X4),
                        lhsT_scale=w4_planes[a][:, b * PASS + t * P : b * PASS + (t + 1) * P],
                        rhs=v_words[a][:, picked].bitcast(FP8X4),
                        rhs_scale=v_planes[a][:, picked],
                        start=(a == 0),
                        stop=(a == PASSES - 1),
                    )
            return lin

        def gated(b, j, lin):
            quarter, half = divmod(j, 2)
            nc.vector.tensor_tensor(
                h_of(b, j * BLOCK, BLOCK).rearrange("p n (u e) -> p n u e", e=2),
                lin[:].rearrange("p (u e) n -> p n u e", e=2),
                soft[quarter][:, :, half * BLOCK : (half + 1) * BLOCK, :].rearrange("p u n e -> p n u e"),
                ALU.mult,
            )

        def quantize_h(b, first, width):
            nc.vector.quantize_mx(
                out=h_codes[:, b, first : first + width].bitcast(FP8X4),
                scales=h_scale[:, b, first : first + width],
                in_=h_of(b, first, width).rearrange("p n t -> p (n t)"),
            )

        def rates(first, width, banks, counts=None):
            cols = slice(first, first + width)
            tiles_in_bank = PACK // len(banks)
            counts = held([P, PACK, width], F32, "counts%d" % first) if counts is None else counts
            ys = [bank(k, [P, tiles_in_bank, width]) for k in banks]
            for b in range(PASSES):
                for i in range(PACK):
                    group, e = divmod(i, tiles_in_bank)
                    nc.tensor.matmul_mx(
                        out=ys[group][:, e, :],
                        lhsT=v2_words[b][:, i * P : (i + 1) * P].bitcast(FP8X4),
                        lhsT_scale=v2_scale[:].bitcast(U8)[4 * b :, i * P : (i + 1) * P],
                        rhs=h_codes[:, b, cols].bitcast(FP8X4),
                        rhs_scale=h_scale[:, b, cols],
                        start=(b == 0 and e == 0),
                        stop=(b == PASSES - 1 and e == tiles_in_bank - 1),
                    )
            for i in range(PACK):
                group, e = divmod(i, tiles_in_bank)
                nc.scalar.activation(counts[:, i, :], ys[group][:, e, :], ACT.Exp, bias=bias[:, i : i + 1])
            return counts

        def expose(first, width, counts, engine, tiles, stored, queue, low_tile=0, high_tile=PACK):
            cols = slice(first, first + width)
            for i in range(low_tile, high_tile, tiles):
                part = counts[:, i : i + tiles, :]
                engine.tensor_tensor(part, part, exposure[:, cols].unsqueeze(1).to_broadcast([P, tiles, width]), ALU.mult)
                if (i + tiles) % stored == 0:
                    low = i + tiles - stored
                    queue.dma_start(
                        out[low * P : (low + stored) * P, cols].rearrange("(i p) n -> p i n", p=P),
                        counts[:, low : low + stored, :],
                    )

        zs = [bank(k, [P, 2, QUARTER]) for k in range(BANKS)]
        for k in range(BANKS):
            logit_pass(zs[k], 0, k, 0)
        for k in range(BANKS):
            logit_pass(zs[k], 0, k, 1)
            sigmoid(0, k, zs[k])
        round_w1(raw01, 0, 1, nc.vector.tensor_copy)
        quantize_w1(0, 1)
        round_w1(raw11, 1, 1, nc.vector.tensor_copy)
        quantize_w1(1, 1)
        w4_codes.append(held([P, PASSES, PACK, 2 * P], U8, "w1_bf16_11"))
        nc.vector.tensor_copy(
            w4_codes[0][:].bitcast(U16).rearrange("p a t (m i) -> p a m t i", i=8),
            w4_raw[:, :, 0 : H // 4].bitcast(U16).rearrange("p a (m i t) -> p a m t i", t=PACK, i=8),
        )

        def gather_v2(c):
            nc.vector.tensor_copy(v2_words[c][:], tab2[c].bitcast(U32).indirect(perils[:]))

        v2_words = [held([P, S2], U32, "v2_words0")]
        gather_v2(0)
        w4_codes.append(placed([P, PASSES, PACK, 2 * P], U8, "w4_codes1", 4))
        for a in range(PASSES):
            for u in range(2):
                nc.gpsimd.tensor_copy(
                    w4_codes[1][:, a, 2 * u : 2 * u + 2, :].rearrange("p t (m y) -> p t m y", y=2),
                    w4_raw[:, a, H // 4 :].bitcast(U8).rearrange("p (m t y) -> p t m y", t=PACK, y=2)[:, 2 * u : 2 * u + 2],
                )
        soft = [placed([P, 2, QUARTER, 2], F32, "soft%d" % quarter, quarter) for quarter in range(4)]

        def logits(b, unit, k):
            z = bank(k, [P, 2, QUARTER])
            for a in range(PASSES):
                logit_pass(z, b, unit, a)
            return z

        def maximum(b, k):
            softplus(b, k, zs[k])
            again = k - REPEAT_AFTER[b]
            if 0 <= again < len(AGAIN[b]):
                repeated = AGAIN[b][again]
                z_bank[repeated] = z_bank[k]
                zs[repeated] = logits(b, repeated, z_bank[k])
            else:
                lin_bank.append(z_bank[k])
                lins.append(linear(b, len(lins), z_bank[k]))

        z_bank = list(range(BANKS))
        lin_bank = list(AGAIN[0])
        lins = [linear(0, j, k) for j, k in enumerate(lin_bank)]
        logs(0)
        following = {}

        def next_logits(k, place):
            following[k] = (logits(1, k, place), place)
            sigmoid(1, k, following[k][0])

        for n in range(4):
            maximum(0, n)
        gated(0, 0, lins[0])
        next_logits(4, 6)
        maximum(0, 4)
        gated(0, 1, lins[1])
        next_logits(5, 7)
        softplus(0, 5, zs[5])
        next_logits(0, 5)
        softplus(0, 6, zs[6])
        next_logits(1, 0)
        gated(0, 2, lins[2])
        next_logits(2, 2)
        softplus(0, 7, zs[7])
        next_logits(3, 1)
        next_logits(6, 6)
        next_logits(7, 7)
        gated(0, 3, lins[3])
        lins.append(linear(0, 5, 3))
        gated(0, 4, lins[4])
        lins.append(linear(0, 6, 4))
        v2_words.append(placed([P, S2], U32, "v2_words1", 1))
        gather_v2(1)
        gated(0, 5, lins[5])
        lins.append(linear(0, 7, 3))
        quantize_h(0, 0, HALF)
        gated(0, 6, lins[6])
        quantize_h(0, HALF, QUARTER)
        gated(0, 7, lins[7])
        quantize_h(0, HALF + QUARTER, QUARTER)
        whole = held([P, 4, 2, QUARTER, 2], F32, "reused1")
        soft = [whole[:, quarter] for quarter in range(4)]

        zs = {k: following[k][0] for k in range(BANKS)}
        lins = [linear(1, 0, 4), linear(1, 1, 3)]
        logs(1)
        pieces = [(0, QUARTER), (QUARTER, QUARTER), (2 * QUARTER, QUARTER), (6 * BLOCK, BLOCK), (7 * BLOCK, BLOCK)]
        done = []

        softplus(1, 0, zs[0])
        lins.append(linear(1, 2, 5))
        softplus(1, 1, zs[1])
        lins.append(linear(1, 3, 0))
        gated(1, 0, lins[0])
        zs[4] = logits(1, 4, 4)
        gated(1, 1, lins[1])
        zs[5] = logits(1, 5, 3)
        softplus(1, 2, zs[2])
        quantize_h(1, *pieces[0])
        softplus(1, 3, zs[3])
        done.append(rates(*pieces[0], [2, 1]))
        gated(1, 2, lins[2])
        lins.append(linear(1, 4, 5))
        gated(1, 3, lins[3])
        lins.append(linear(1, 5, 0))
        softplus(1, 4, zs[4])
        lins.append(linear(1, 6, 4))
        quantize_h(1, *pieces[1])
        softplus(1, 5, zs[5])
        lins.append(linear(1, 7, 3))
        gated(1, 4, lins[4])
        softplus(1, 6, zs[6])
        done.append(rates(*pieces[1], [5, 6]))
        softplus(1, 7, zs[7])
        gated(1, 5, lins[5])
        gated(1, 6, lins[6])
        quantize_h(1, *pieces[2])
        done.append(rates(*pieces[2], [7, 0]))
        shifted = [held([P, 2, QUARTER], F32, "h1_1")[:], done[0][:, 0:2, :]]
        for n in range(2):
            factor = exposure[:, 0:QUARTER].unsqueeze(1).to_broadcast([P, 2, QUARTER])
            nc.gpsimd.tensor_tensor(shifted[n], done[0][:, 2 * n : 2 * n + 2, :], factor, ALU.mult)
            nc.sync.dma_start(out[2 * n * P : (2 * n + 2) * P, 0:QUARTER].rearrange("(i p) n -> p i n", p=P), shifted[n])
        quantize_h(1, *pieces[3])
        last = held([P, PACK, QUARTER], F32, "counts_last")
        rates(*pieces[3], [2, 1], last[:, :, 0:BLOCK])
        gated(1, 7, lins[7])
        expose(*pieces[1], done[1], nc.vector, 2, 2, nc.sync, 0, 2)
        quantize_h(1, *pieces[4])
        rates(*pieces[4], [4, 5, 6, 3], last[:, :, BLOCK:])
        expose(*pieces[1], done[1], nc.vector, 2, 2, nc.sync, 2, 4)
        expose(*pieces[2], done[2], nc.vector, 2, 2, nc.sync)
        expose(3 * QUARTER, QUARTER, last, nc.vector, 2, 2, nc.sync, 0, 2)
        expose(3 * QUARTER, QUARTER, last, nc.vector, 1, 1, nc.sync, 2, 4)
